import numpy as np, ml_dtypes
CORES = [2,3,42,43,82,83,122,123]
N = 8
BF = ml_dtypes.bfloat16
def gentries(a):
    return np.ascontiguousarray(a.reshape(8, 16, -1).transpose(0, 2, 1)).reshape(8, -1)
def gtable(e):
    e = np.asarray(e); return np.ascontiguousarray(e.reshape(8, -1, 16).transpose(0, 2, 1)).reshape(128, -1).astype(np.int32)
P, A, M, Q = 32768, 4, 8, 256
S = N * P
def letters(rng, w, n):
    a = np.add.accumulate(w); return np.searchsorted(a[:-1], rng.random(n) * a[-1], side="right")
def places(rng):
    p = rng.integers(0, S + 1, (N, 8, 2, Q)); u = P // 8
    v = rng.integers(0, 8 * N + 1, p.shape) * u + rng.integers(-1, 2, p.shape)
    p = np.sort(np.where(rng.random(p.shape) < 0.25, np.minimum(np.maximum(v, 0), S), p), axis=2)
    k = (8 * np.arange(N)[:, None] + np.arange(8)) * u
    p[:, :, 0, Q - 5] = k; p[:, :, 1, Q - 5] = k + u; p[:, :, :, Q - 4] = S; p[:, :, :, Q - 3] = 0
    p[:, :, 1, Q - 2] = p[:, :, 0, Q - 2]; p[:, :, 0, Q - 1] = 0; p[:, :, 1, Q - 1] = S
    return p
def pack(s, e, p):
    return {"bwt": np.ascontiguousarray(np.asarray(s).reshape(8, N, P).transpose(1, 0, 2)).astype(np.int32), "pats": np.stack([gtable(e[r].reshape(8, M * Q)) for r in range(N)]), "starts": np.stack([gtable(p[r].reshape(8, 2 * Q)) for r in range(N)])}
def bw(t):
    n = len(t); key = np.zeros(n, np.int64); k = 62 // (A - 1).bit_length()
    for i in range(k): key = key * A + np.roll(t, -i)
    while True:
        o = np.argsort(key); ks = key[o]
        v = np.zeros(n, np.int64); v[o[1:]] = np.add.accumulate((ks[1:] != ks[:-1]).astype(np.int64))
        if v.max() == n - 1 or k >= n: break
        key = (v * n + np.roll(v, -k)) * n + np.roll(v, -2 * k); k *= 3
    return t[o - 1]
def setup_inputs(rng):
    s = []; e = rng.integers(0, A, (N, 8, M, Q)); h = Q // 2
    for g in range(8):
        w = np.exp2(rng.integers(0, 4, A)); c = rng.integers(0, A); w[c] += 4 * A
        s.append(np.concatenate([letters(rng, w * np.exp2(rng.integers(0, 3, A)), P) for r in range(N)]))
        e[:, g, :, :h] = np.where(rng.random((N, M, h)) < 0.875, c, e[:, g, :, :h])
    return pack(np.stack(s), e, places(rng))
def setup_inputs_ends(rng):
    i = np.arange(S); s = np.zeros((8, S), np.int64)
    s[0] = i * A // S; s[1] = A - 1 - s[0]; s[2] = i % A; s[3] = rng.integers(0, A - 1, S); s[4] = rng.integers(1, A, S); s[5] = i // P % A
    s[6] = np.where((i % P == 0) | (i % P == P - 1), A - 1, rng.integers(0, A - 1, S)); s[7] = np.where(i == S - 1, A - 1, rng.integers(0, A - 1, S))
    e = rng.integers(0, A, (N, 8, M, Q)); e[..., 0] = 0; e[..., 1] = A - 1; e[..., 2] = 0; e[:, :, 0, 2] = A - 1; e[..., 3] = 0; e[:, :, M - 1, 3] = A - 1
    q = rng.integers(0, N); e[q] = rng.integers(0, A, (8, M, 1)); e[q, 0] = e[q, 0, 0, 0]
    p = places(rng); p[:, :, 0, :4] = 0; p[:, :, 1, :4] = S; p[q, :, 0] = 0; p[q, :, 1] = S
    return pack(s, e, p)
def setup_inputs_one(rng):
    k = (np.arange(8) + rng.integers(0, A)) % A; c = k[None, :, None, None]
    e = np.where(rng.random((N, 8, 1, Q)) < 0.5, c, rng.integers(0, A, (N, 8, M, Q))); e[..., 0] = k[None, :, None]
    return pack(np.repeat(k[:, None], S, axis=1), e, places(rng))
def setup_inputs_text(rng):
    s = []; e = np.zeros((N, 8, M, Q), np.int64); h = Q // 2
    for g in range(8):
        t = np.tile(letters(rng, np.exp2(rng.integers(0, 3, A)), S // 8), 8); t = np.where(rng.random(S) < 0.03125, rng.integers(0, A, S), t); s.append(bw(t))
        e[:, g] = t[(rng.integers(0, S, (N, 1, Q)) + (M - 1 - np.arange(M))[None, :, None]) % S]
    e[..., h:] = np.where(rng.random((N, 8, M, Q - h)) < 0.0625, rng.integers(0, A, (N, 8, M, Q - h)), e[..., h:])
    p = places(rng); p[:, :, 0, :h] = 0; p[:, :, 1, :h] = S
    return pack(np.stack(s), e, p)
def setup_inputs_spread(rng):
    s = np.stack([np.concatenate([letters(rng, np.exp2(-2.0 * rng.permutation(A)), P) for r in range(N)]) for g in range(8)])
    e = np.stack([s[g][rng.integers(0, S, (N, M, Q))] for g in range(8)], axis=1)
    p = places(rng); p[:, :, 1] = np.minimum(p[:, :, 0] + (rng.integers(0, S + 1, (N, 8, Q)) >> rng.integers(0, 20, (N, 8, Q))), S)
    return pack(s, np.where(rng.random((N, 8, 1, Q)) < 0.5, e, rng.integers(0, A, (N, 8, M, Q))), p)
def check_inputs(d):
    bad = [k + " out of range" for k in ("bwt", "pats") if not ((d[k] >= 0) & (d[k] < A)).all()]
    if not ((d["starts"] >= 0) & (d["starts"] <= S)).all(): bad.append("starts out of range")
    p = np.stack([gentries(a) for a in d["starts"]]).reshape(N, 8, 2, Q)
    if (p[:, :, 0] > p[:, :, 1]).any(): bad.append("lo over hi in starts")
    return bad
def reference(bwt, pats, starts):
    s = bwt.transpose(1, 0, 2).reshape(8, S)
    e = np.stack([gentries(pats[r]) for r in range(N)]).reshape(N, 8, M, Q)
    b = np.stack([gentries(starts[r]) for r in range(N)]).reshape(N, 8, 2, Q).astype(np.int64)
    ends = np.zeros((N, 8, 2, Q), np.int64)
    for g in range(8):
        C = np.array([np.count_nonzero(s[g] < c) for c in range(A)]); occ = np.zeros((A, S + 1), np.int64)
        for c in range(A): occ[c, 1:] = np.add.accumulate((s[g] == c).astype(np.int64))
        p = b[:, g]
        for t in range(M):
            c = e[:, g, t][:, None]; p = C[c] + occ[c, p]
        ends[:, g] = p
    return {"y": np.asarray(np.stack([gtable(ends[r].reshape(8, 2 * Q)) for r in range(N)]), np.float32)}

@@ -1,0 +1,310 @@
+import numpy as np
+from concourse.bass import DstId, RemoteDMATransfer
+from concourse.mybir import AluOpType as A, AxisListType, ActivationFunctionType as AF
+
+NPE = 4
+OFFS = 49152.0
+B_T = (0.0, 638.5, 2552.5, 10208.5)
+
+SCRATCH = {
+    "PP": ("dram", [8, 128, 16], "int32"), "SS": ("dram", [8, 128, 4], "int32"),
+    "PL": ("dram", [8, 128, 16], "int32"), "SL": ("dram", [8, 128, 4], "int32"),
+    "FL": ("dram", [8, 128, 32], "float32"),
+    "PSA": ("psum", [128, 2048], "float32"), "PSB": ("psum", [128, 2048], "float32"),
+}
+for _n, _w, _d in (
+        ("D32", 2048, "int32"), ("D", 2048, "bfloat16"), ("CE", 2048, "bfloat16"), ("SENDX", 512, "bfloat16"),
+        ("SENDC", 128, "float32"), ("LX", 512, "bfloat16"), ("LC", 128, "float32"), ("LXP", 512, "bfloat16"),
+        ("TA", 2048, "bfloat16"), ("TB", 2048, "bfloat16"), ("CI", 128, "int32"), ("CX", 512, "int32"), ("NS", 512, "float32"),
+        ("S1", 512, "bfloat16"), ("N15", 32, "bfloat16"), ("MK", 512, "float32"), ("BASE", 40, "float32"),
+        ("ONE32", 32, "float32"), ("F", 512, "float32"), ("HNS", 512, "float32"), ("NI", 512, "int32"), ("DI", 2048, "int32"),
+        ("DB", 2048, "bfloat16"), ("XL", 2048, "bfloat16"), ("XC", 2048, "bfloat16"), ("X", 16400, "bfloat16"),
+        ("ONESB", 2048, "bfloat16"), ("ID", 128, "bfloat16"), ("IDN", 128, "bfloat16"), ("PK", 512, "bfloat16"),
+        ("HK", 512, "bfloat16"), ("TRI", 128, "bfloat16"), ("SEL", 1024, "bfloat16"), ("LA", 2048, "bfloat16"),
+        ("LB", 2048, "bfloat16"), ("LR", 2048, "bfloat16"), ("KI", 8, "int32"), ("KF", 32, "float32"), ("G1", 64, "float32"),
+        ("G2", 64, "float32"), ("G3", 64, "float32"), ("G4", 32, "float32"), ("G5", 32, "float32"), ("IC4", 4, "float32"),
+        ("EM", 8, "float32"), ("EV", 8, "float32"), ("EI", 4, "int32"), ("W", 64, "bfloat16"), ("C4", 16, "bfloat16"),
+        ("OFX", 32, "uint16"), ("OFF", 32, "uint16"), ("PT", 128, "int32"), ("ST", 32, "int32"), ("ST4", 32, "int32"),
+        ("OFP", 128, "uint16"), ("QT", 128, "bfloat16"), ("CM", 2048, "bfloat16"), ("RES", 32, "float32"),
+        ("I0", 16, "int32"), ("J0", 32, "int32"), ("O0", 32, "uint16"), ("Z0", 256, "bfloat16"), ("Y0", 256, "bfloat16"), ("E0", 256, "bfloat16"),
+        ("I1", 16, "int32"), ("J1", 32, "int32"), ("O1", 32, "uint16"), ("Z1", 256, "bfloat16"), ("Y1", 256, "bfloat16"), ("E1", 256, "bfloat16")):
+    SCRATCH[_n] = ("sbuf", [128, _w], _d)
+SEMAPHORES = (["vq", "aq", "pq", "gq", "dp", "ds", "dsp", "dss", "lpt", "lst", "rep", "yself", "yout",
+               "arrP", "arrS", "arrX", "arrC", "arrF", "locP", "locS", "locX", "locC", "locF"] + ["b%d" % _i for _i in range(8)])
+
+
+def rank_program(g, core, T, topo):
+    rank = T.rank_of(core)
+    if rank is None:
+        return
+    Q = {"v": g.vector, "a": g.scalar, "p": g.tensor, "g": g, "s": g.sync}
+    QS = {"v": "vq", "a": "aq", "p": "pq", "g": "gq"}
+    total, last, readers = {}, {}, {}
+    known = {q: {} for q in Q}
+
+    def wait(q, tok):
+        sem, val, know = tok
+        if val is None:
+            val = total[sem]
+        if known[q].get(sem, 0) >= val:
+            return
+        Q[q].wait_ge(T.sem[sem], int(val))
+        known[q][sem] = val
+        for s, v in know.items():
+            if known[q].get(s, 0) < v:
+                known[q][s] = v
+
+    def deps(q, rd, wr):
+        own = QS.get(q)
+        for k in rd:
+            if k in last:
+                wait(q, last[k])
+        for k in wr:
+            for tok in readers.get(k, []) + ([last[k]] if k in last else []):
+                if tok[0] != own:
+                    wait(q, tok)
+
+    def mark(tok, rd, wr):
+        for k in rd:
+            readers.setdefault(k, []).append(tok)
+        for k in wr:
+            last[k] = tok
+            readers[k] = []
+
+    def op(q, name, args, rd, wr, **kw):
+        deps(q, rd, wr)
+        o = Q[q]
+        fn = {"copy": lambda: o.tensor_copy(*args), "tt": lambda: o.tensor_tensor(*args), "ts": lambda: o.tensor_scalar(*args),
+              "memset": lambda: o.memset(*args), "red": lambda: o.tensor_reduce(*args), "scan": lambda: o.tensor_tensor_scan(*args),
+              "act": lambda: o.activation(*args, **kw), "iota": lambda: o.iota(*args, **kw), "asel": lambda: o.affine_select(*args)}[name]
+        s = QS[q]
+        fn().then_inc(T.sem[s], 1)
+        total[s] = total.get(s, 0) + 1
+        mark((s, total[s], dict(known[q])), rd, wr)
+
+    def mms(calls, rd, wr):
+        deps("p", rd, wr)
+        for i, a in enumerate(calls):
+            ins = g.tensor.matmul(*a)
+            if i == len(calls) - 1:
+                ins.then_inc(T.sem.pq, 1)
+        total["pq"] = total.get("pq", 0) + 1
+        mark(("pq", total["pq"], dict(known["p"])), rd, wr)
+
+    def dma(q, out, in_, sem, rd, wr):
+        deps(q, rd, wr)
+        Q[q].dma_start(out, in_).then_inc(T.sem[sem], 16)
+        total[sem] = total.get(sem, 0) + 16
+        mark((sem, None, dict(known[q])), rd, wr)
+
+    def send(src, dst, arr, loc, rd):
+        deps("g", rd, [])
+        tr, used = [], set()
+        peers = sorted([d for d in range(8) if d != rank], key=lambda d: len(topo.engines(core, T.cores[d])))
+        for d in peers:
+            dc = T.cores[d]
+            e = [e for e in topo.engines(core, dc) if e not in used][0]
+            used.add(e)
+            rid, pid, _ = topo.addr(dc)
+            tr.append(RemoteDMATransfer(dst_ids=[DstId(rid=rid, pnc=pid)], dma_engine_mask=1 << e, remote_sem=T.sem[arr], srcs=[src(d)], dsts=[dst]))
+        g.remote_dma_fused(tr, local_sem=T.sem[loc])
+        total[loc] = 7
+        total[arr] = 7
+        mark((loc, 7, dict(known["g"])), rd, [])
+
+    V = lambda name, args, rd, wr: op("v", name, args, rd, wr)
+    for k, arr in (("PL", "arrP"), ("SL", "arrS"), ("LX", "arrX"), ("LC", "arrC"), ("FL", "arrF")):
+        last[k] = (arr, 7, {})
+
+    dma("s", T.PP[:], T.pats[:], "dp", [], ["PP"])
+    dma("s", T.SS[:], T.starts[:], "ds", [], ["SS"])
+    for s in range(8):
+        dma("s" if s % 2 == 0 else "a", T.D32[:, 256 * s:256 * s + 256], T.bwt[s:s + 1, :], "b%d" % s, [], ["D32%d" % s])
+    dma("s", T.PL[rank], T.pats[16 * rank:16 * rank + 16, :], "dsp", [], ["PLs"])
+    dma("s", T.SL[rank], T.starts[16 * rank:16 * rank + 16, :], "dss", [], ["SLs"])
+    V("memset", (T.ONESB[:], 1.0), [], ["ONESB"])
+    op("g", "asel", (T.ID[:], T.ONESB[:, 0:128], [[-1, 128]], A.is_equal, 0.0, 0, 1), ["ONESB"], ["ID"])
+    for i in range(4):
+        V("ts", (T.PK[:, 128 * i:128 * i + 128], T.ID[:], float(4 ** i), None, A.mult), ["ID"], ["PK"])
+    send(lambda d: T.PP[d], T.PL[rank], "arrP", "locP", ["PP"])
+    send(lambda d: T.SS[d], T.SL[rank], "arrS", "locS", ["SS"])
+
+    CH = 5.0 * float(np.log(2.0))
+    for hh in range(2):
+        for s in range(4 * hh, 4 * hh + 4):
+            c0 = 256 * s
+            V("copy", (T.D[:, c0:c0 + 256], T.D32[:, c0:c0 + 256]), ["D32%d" % s], ["D%d" % s])
+            op("a", "act", (T.CE[:, c0:c0 + 256], T.D[:, c0:c0 + 256], AF.Exp), ["D%d" % s], ["CE%d" % s], scale=CH)
+        lo, hi = 1024 * hh, 1024 * hh + 1024
+        mms([(T.PSA[:, 512 * hh:512 * hh + 256], T.PK[:, 128 * i:128 * i + 128], T.D[:, lo + i:hi:4], i == 0, i == 3) for i in range(4)],
+            ["D%d" % s for s in range(4 * hh, 4 * hh + 4)] + ["PK"], ["A%d" % hh])
+        V("copy", (T.SENDX[:, 256 * hh:256 * hh + 256], T.PSA[:, 512 * hh:512 * hh + 256]), ["A%d" % hh], ["A%d" % hh, "SENDX%d" % hh])
+    send(lambda d: T.SENDX[:, 64 * d:64 * d + 64], T.LX[:, 64 * rank:64 * rank + 64], "arrX", "locX", ["SENDX0", "SENDX1"])
+    for hh in range(2):
+        lo, hi, o = 1024 * hh, 1024 * hh + 1024, 1024 + 512 * hh
+        mms([(T.PSA[:, o:o + 64], T.ID[:], T.CE[:, lo + q:hi:16], q == 0, q == 15) for q in range(16)],
+            ["CE%d" % s for s in range(4 * hh, 4 * hh + 4)] + ["ID"], ["A%d" % (2 + hh)])
+        V("copy", (T.SENDC[:, 64 * hh:64 * hh + 64], T.PSA[:, o:o + 64]), ["A%d" % (2 + hh)], ["A%d" % (2 + hh), "SENDC%d" % hh])
+    send(lambda d: T.SENDC[:, 16 * d:16 * d + 16], T.LC[:, 16 * rank:16 * rank + 16], "arrC", "locC", ["SENDC0", "SENDC1"])
+    h = rank // 4
+    V("copy", (T.LX[:, 64 * rank:64 * rank + 64], T.SENDX[:, 64 * rank:64 * rank + 64]), ["SENDX%d" % h], ["LXs"])
+    V("copy", (T.LC[:, 16 * rank:16 * rank + 16], T.SENDC[:, 16 * rank:16 * rank + 16]), ["SENDC%d" % h], ["LCs"])
+
+    fl = dict(allow_small_or_imprecise_dtypes=True)
+    op("g", "iota", (T.KI[:, 0:1], [[0, 1]], 0, 1), [], ["KI0"])
+    op("g", "iota", (T.G4[:], [[4, 16], [256, 2]], 0, 0), [], ["G4"], **fl)
+    op("g", "iota", (T.G5[:], [[1, 16], [64, 2]], 0, 0), [], ["G5"], **fl)
+    op("g", "iota", (T.G1[:], [[1, 16], [0, 4]], 0, 0), [], ["G1"], **fl)
+    op("g", "iota", (T.G2[:], [[0, 16], [32, 4]], 6144, 0), [], ["G2"], **fl)
+    op("g", "iota", (T.IC4[:], [[1, 4]], 0, 0), [], ["IC4"], **fl)
+    op("g", "asel", (T.TRI[:], T.ONESB[:, 0:128], [[1, 128]], A.is_ge, 0.0, -1, -1), ["ONESB"], ["TRI"])
+    op("g", "asel", (T.SEL[:], T.ONESB[:, 0:1024], [[-16, 8], [0, 8], [-1, 16]], A.is_equal, 0.0, 0, 1), ["ONESB"], ["SEL"])
+    op("g", "asel", (T.LA[:], T.ONESB[:], [[-1, 16], [0, 8], [1, 16]], A.is_equal, 0.0, 0, 0), ["ONESB"], ["LA"])
+    op("g", "asel", (T.LB[:], T.LA[:], [[0, 16], [-16, 8], [0, 16]], A.is_ge, 0.0, 0, 1), ["LA"], ["LB"])
+    op("g", "asel", (T.LR[:], T.LB[:], [[0, 16], [16, 8], [0, 16]], A.is_ge, 0.0, 15, -1), ["LB"], ["LR"])
+    for d, n, sh in ((1, 15, 0), (2, 3, 0), (3, 3, 2), (4, 1, 0), (5, 1, 1)):
+        V("ts", (T.KI[:, d:d + 1], T.KI[:, 0:1], sh, n, A.arith_shift_right, A.bitwise_and), ["KI0"], ["KI"])
+    V("copy", (T.KF[:, 0:6], T.KI[:, 0:6]), ["KI", "KI0"], ["KF"])
+    col = lambda j: T.KF[:, j:j + 1]
+    V("ts", (col(19), col(3), 64.0, None, A.mult), ["KF"], ["K19"])
+    V("tt", (col(20), col(19), col(2), A.add), ["K19", "KF"], ["K20"])
+    V("ts", (T.OFX[:], T.G4[:], col(20), None, A.add), ["G4", "K20"], ["OFX"])
+    V("ts", (col(13), col(4), -5120.0, 20480.0, A.mult, A.add), ["KF"], ["K13"])
+    V("tt", (col(14), col(4), col(5), A.mult), ["KF"], ["K14"])
+    V("ts", (col(15), col(14), -15360.0, None, A.mult), ["K14"], ["K15"])
+    V("ts", (col(16), col(5), -5120.0, None, A.mult), ["KF"], ["K16"])
+    V("tt", (col(17), col(13), col(15), A.add), ["K13", "K15"], ["K17"])
+    V("tt", (col(18), col(17), col(16), A.add), ["K17", "K16"], ["K18"])
+    V("ts", (col(6), col(4), 31.0, 1.0, A.mult, A.add), ["KF"], ["K6"])
+    V("ts", (col(7), col(5), 1023.0, 1.0, A.mult, A.add), ["KF"], ["K7"])
+    V("tt", (col(8), col(6), col(7), A.mult), ["K6", "K7"], ["K8"])
+    V("ts", (col(9), col(4), -31.0 / 32, 1.0, A.mult, A.add), ["KF"], ["K9"])
+    V("ts", (col(10), col(5), -1023.0 / 1024, 1.0, A.mult, A.add), ["KF"], ["K10"])
+    V("tt", (col(11), col(9), col(10), A.mult), ["K9", "K10"], ["K11"])
+    V("ts", (col(12), col(11), 0.5, -0.5, A.mult, A.add), ["K11"], ["K12"])
+    V("ts", (col(21), col(2), 128.0, None, A.mult), ["KF"], ["K21"])
+    V("ts", (col(22), col(3), 16.0, None, A.mult), ["KF"], ["K22"])
+    V("tt", (col(23), col(21), col(22), A.add), ["K21", "K22"], ["K23"])
+    V("ts", (T.OFF[:], T.G5[:], col(23), None, A.add), ["G5", "K23"], ["OFF"])
+    V("ts", (T.G3[:], T.G1[:], col(1), None, A.is_gt), ["G1", "KF"], ["G3"])
+    V("tt", (T.W[:], T.G3[:], T.G2[:], A.mult), ["G3", "G2"], ["W"])
+    V("ts", (T.C4[:, 0:4], T.IC4[:], col(3), col(8), A.is_equal, A.mult), ["IC4", "KF", "K8"], ["C4"])
+    V("ts", (T.EM[:, 0:4], T.IC4[:], col(3), None, A.is_equal), ["IC4", "KF"], ["EM"])
+    V("memset", (T.MK[:], 1.0), [], ["MK0"])
+    V("memset", (T.MK[:, 0:512:16], 0.0), ["MK0"], ["MK"])
+    V("memset", (T.ONE32[:], 1.0), [], ["ONE32"])
+    V("memset", (T.BASE[:, 0:1], 0.0), [], ["BASE0"])
+    V("memset", (T.TB[:, 3:2048:4], 0.0), [], ["TB3"])
+    V("ts", (T.IDN[:], T.ID[:], -1.0, None, A.mult), ["ID"], ["IDN"])
+    for i, k in enumerate((-1.0, -28.0, -896.0, 4096.0)):
+        V("ts", (T.HK[:, 128 * i:128 * i + 128], T.ID[:], k, None, A.mult), ["ID"], ["HK"])
+    dma("s", T.PT[:], T.PL[:], "lpt", ["PL", "PLs"], ["PT"])
+    dma("s", T.ST[:], T.SL[:], "lst", ["SL", "SLs"], ["ST"])
+    V("copy", (T.OFP[:], T.PT[:]), ["PT"], ["OFP"])
+    V("ts", (T.QT[:], T.PT[:], 0.25, None, A.mult), ["PT"], ["QT"])
+    V("ts", (T.ST4[:], T.ST[:], 4.0, None, A.mult), ["ST"], ["ST4"])
+    for h in range(2):
+        V("tt", (T["I%d" % h][:], T.ST4[:, 16 * h:16 * h + 16], T.PT[:, 0:16], A.add), ["ST4", "PT"], ["I%d" % h])
+
+    TAK, TBK = ["TA0", "TA1", "TA2", "TA3"], ["TB0", "TB1", "TB2", "TB3"]
+    op("a", "act", (T.LXP[:], T.LX[:, 0:512].indirect(T.OFX[:, 0:32]), AF.Copy), ["LX", "LXs", "OFX"], ["LXP"])
+    for i in range(1, 4):
+        V("ts", (T.TA[:, i:2048:4], T.LXP[:], B_T[i], 32.0 / 4 ** i, A.add, A.mult), ["LXP"], ["TA%d" % i])
+    op("a", "act", (T.TA[:, 0:2048:4], T.LXP[:], AF.Identity), ["LXP"], ["TA0"], scale=32.0)
+    mms([(T.PSB[:, 0:512], T.HK[:, 128 * i:128 * i + 128], T.TA[:, i:2048:4], i == 0, i == 3) for i in range(4)], TAK + ["HK"], ["B0"])
+    for i in range(3):
+        sc = 32.0 / 4 ** i
+        op("a", "act", (T.TB[:, i:2048:4], T.LXP[:], AF.Copy), ["LXP"], ["TB%d" % i], scale=sc, bias=sc * B_T[i + 1])
+    op("a", "act", (T.HNS[:], T.PSB[:, 0:512], AF.Copy), ["B0"], ["B0", "HNS"])
+    for bk in range(4):
+        cs = []
+        for il in range(4 * bk, 4 * bk + 4):
+            o = T.PSA[:, 128 * il:128 * il + 128]
+            cs += [(o, T.TA[:, 128 * il:128 * il + 128], T.ID[:], True, False), (o, T.TB[:, 128 * il:128 * il + 128], T.IDN[:], False, True)]
+        mms(cs, TAK + TBK + ["ID", "IDN"], ["A%d" % bk])
+        op("a", "act", (T.XL[:, 512 * bk:512 * bk + 512], T.PSA[:, 512 * bk:512 * bk + 512], AF.Identity), ["A%d" % bk, "K18"],
+           ["A%d" % bk, "XL%d" % bk], bias=col(18))
+    op("a", "act", (T.CM[:], T.C4[:, 0:4].indirect(T.OFP[:, 0:128]), AF.Copy), ["C4", "OFP"], ["CM"])
+
+    V("copy", (T.CI[:], T.LC[:]), ["LC", "LCs"], ["CI"])
+    for c in range(4):
+        V("ts", (T.CX[:, 128 * c:128 * c + 128], T.CI[:], 5 * c, 31, A.arith_shift_right, A.bitwise_and), ["CI"], ["CX"])
+    V("copy", (T.NS[:, 1:512], T.CX[:, 0:511]), ["CX"], ["NS"])
+    V("copy", (T.N15[:], T.CX[:, 15:512:16]), ["CX"], ["N15"])
+    V("memset", (T.NS[:, 0:512:16], 0.0), ["NS"], ["NS"])
+    V("scan", (T.S1[:], T.MK[:], T.NS[:], 0.0, A.mult, A.add), ["MK", "NS"], ["S1"])
+    for j, (m, k) in enumerate(((T.ONESB[:, 0:128], "ONESB"), (T.TRI[:], "TRI"))):
+        o = T.PSB[:, 512 + 512 * j:544 + 512 * j]
+        mms([(o, m, T.S1[:, 15:512:16], True, False), (o, m, T.N15[:], False, True)], ["S1", "N15", k], ["B%d" % (1 + j)])
+    V("scan", (T.BASE[:, 1:33], T.ONE32[:], T.PSB[:, 512:544], 0.0, A.mult, A.add), ["B1", "ONE32"], ["B1", "BASE"])
+    V("tt", (T.NS[:, 0:512:16], T.PSB[:, 1024:1056], T.BASE[:, 0:32], A.add), ["B2", "BASE", "BASE0"], ["B2", "NS"])
+    V("scan", (T.F[:], T.MK[:], T.NS[:], 0.0, A.mult, A.add), ["MK", "NS"], ["F"])
+    V("tt", (T.NI[:], T.F[:, 0:512].indirect(T.OFF[:, 0:32]), T.HNS[:], A.add), ["F", "OFF", "HNS"], ["NI"])
+    for i in range(4):
+        V("ts", (T.DI[:, 512 * i:512 * i + 512], T.NI[:], 5 * i, 15 if i == 3 else 31, A.arith_shift_right, A.bitwise_and), ["NI"], ["DI%d" % i])
+    for i in range(4):
+        V("copy", (T.DB[:, i:2048:4], T.DI[:, 512 * i:512 * i + 512]), ["DI%d" % i], ["DB%d" % i])
+    for bk in range(4):
+        mms([(T.PSA[:, 128 * il:128 * il + 128], T.DB[:, 128 * il:128 * il + 128], T.ID[:], True, True) for il in range(4 * bk, 4 * bk + 4)],
+            ["DB0", "DB1", "DB2", "DB3", "ID"], ["A%d" % bk])
+        for il in range(4 * bk, 4 * bk + 4):
+            V("tt", (T.XC[:, il:2048:16], T.PSA[:, 128 * il:128 * il + 128], T.XL[:, 128 * il:128 * il + 128], A.add),
+              ["A%d" % bk, "XL%d" % bk], ["A%d" % bk, "XC"])
+    XK = ["XE"]
+    for k in range(NPE, 8):
+        for y in range(8):
+            dma("s", T.X[16 * y:16 * y + 16, 2048 * k:2048 * k + 2048], T.XC[16 * k:16 * k + 16, :], "rep", ["XC"], ["XD%d%d" % (k, y)])
+            XK.append("XD%d%d" % (k, y))
+    n = 0
+    for k in range(NPE):
+        for j in range(4):
+            b = n % 4
+            mms([(T.PSB[:, 512 * b:512 * b + 512], T.SEL[:, 128 * k:128 * k + 128], T.XC[:, 512 * j:512 * j + 512], True, True)], ["XC", "SEL"], ["B%d" % b])
+            o, x = T.X[:, 2048 * k + 512 * j:2048 * k + 512 * j + 512], T.PSB[:, 512 * b:512 * b + 512]
+            if n % 2 == 0:
+                V("copy", (o, x), ["B%d" % b], ["B%d" % b, "X%d" % n])
+            else:
+                op("a", "act", (o, x, AF.Copy), ["B%d" % b], ["B%d" % b, "X%d" % n])
+            XK.append("X%d" % n)
+            n += 1
+    V("tt", (T.EV[:, 0:4], T.EM[:, 0:4], T.BASE[:, 8:33:8], A.mult), ["EM", "BASE"], ["EV"])
+    V("red", (T.EV[:, 4:5], T.EV[:, 0:4], AxisListType.X, A.add), ["EV"], ["EV4"])
+    V("ts", (T.EV[:, 5:6], T.EV[:, 4:5], 512000.0, col(11), A.add, A.mult), ["EV4", "K11"], ["EV5"])
+    V("ts", (T.EI[:, 0:1], T.EV[:, 5:6], col(12), None, A.add), ["EV5", "K12"], ["EI0"])
+    V("ts", (T.EI[:, 1:2], T.EI[:, 0:1], 31, None, A.bitwise_and), ["EI0"], ["EI1"])
+    V("copy", (T.X[:, 16384:16385], T.EI[:, 1:2]), ["EI1"], ["XE"])
+
+    for t in range(8):
+        for h in range(2):
+            s = str(h)
+            I, J, O, Z, Y, E = (T[x + s] for x in "IJOZYE")
+            ps, pk = T.PSA[:, 512 * h:512 * h + 16], "A" + s
+            if t:
+                V("ts", (I[:], ps, 4.0, OFFS, A.mult, A.add), [pk], [pk, "I" + s])
+            V("ts", (J[:, 0:16], I[:], 6, 0x7FFF, A.arith_shift_right, A.bitwise_and), ["I" + s], ["J" + s])
+            V("ts", (J[:, 16:32], I[:], 63, None, A.bitwise_and), ["I" + s], ["J" + s])
+            V("copy", (O[:], J[:]), ["J" + s], ["O" + s])
+            xb = T.X[:, 0:16385].indirect(O[:, 0:16])
+            op("a", "act", (Z[:], xb, AF.Identity), ["O" + s] + XK, ["Z" + s], bias=6128.5)
+            V("tt", (Y[:], xb, T.CM[:, 256 * t:256 * t + 256], A.mult), ["O" + s, "CM"] + XK, ["Y" + s])
+            V("tt", (E[:], T.W[:, 0:64].indirect(O[:, 16:32]), Z[:], A.is_equal), ["O" + s, "W", "Z" + s], ["E" + s])
+            cs = [(ps, T.LR[:, 128 * r:128 * r + 128], Y[:, r:256:16], r == 0, False) for r in range(16)]
+            if t < 7:
+                cs.append((ps, T.ID[:], T.QT[:, 16 * t + 16:16 * t + 32], False, False))
+            mms(cs, ["Y" + s, "LR", "QT", "ID"], [pk])
+            mms([(ps, T.LR[:, 128 * r:128 * r + 128], E[:, r:256:16], False, r == 15) for r in range(16)], ["E" + s, "LR"], [pk])
+    for h in range(2):
+        s = str(h)
+        ps, pk = T.PSA[:, 512 * h:512 * h + 16], "A" + s
+        V("ts", (T["I" + s][:], ps, 4.0, OFFS, A.mult, A.add), [pk], [pk, "I" + s])
+        V("ts", (T["J" + s][:, 0:16], T["I" + s][:], 2, 0x7FFFF, A.arith_shift_right, A.bitwise_and), ["I" + s], ["J" + s])
+        V("copy", (T.RES[:, 16 * h:16 * h + 16], T["J" + s][:, 0:16]), ["J" + s], ["RES%d" % h])
+    send(lambda d: T.RES[:], T.FL[rank], "arrF", "locF", ["RES0", "RES1"])
+    r0, r1 = 16 * rank, 16 * rank + 16
+    dma("s", T.y[r0:r1, :], T.RES[r0:r1, :], "yself", ["RES0", "RES1"], ["y0"])
+    if rank > 0:
+        dma("s", T.y[0:r0, :], T.FL[0:rank, r0:r1, :], "yout", ["FL"], ["y1"])
+    if rank < 7:
+        dma("s", T.y[r1:128, :], T.FL[rank + 1:8, r0:r1, :], "yout", ["FL"], ["y2"])
+    for sem in sorted(total):
+        wait("g", (sem, total[sem], {}))

@@ -2,8 +2,8 @@ import numpy as np
 from concourse.bass import DstId, RemoteDMATransfer
 from concourse.mybir import AluOpType as A, AxisListType, ActivationFunctionType as AF
 
-NPE = 4
-OFFS = 49152.0
+NPE = 5
+BIAS = 131072
 B_T = (0.0, 638.5, 2552.5, 10208.5)
 
 SCRATCH = {
@@ -19,15 +19,16 @@ for _n, _w, _d in (
         ("S1", 512, "bfloat16"), ("N15", 32, "bfloat16"), ("MK", 512, "float32"), ("BASE", 40, "float32"),
         ("ONE32", 32, "float32"), ("F", 512, "float32"), ("HNS", 512, "float32"), ("NI", 512, "int32"), ("DI", 2048, "int32"),
         ("DB", 2048, "bfloat16"), ("XL", 2048, "bfloat16"), ("XC", 2048, "bfloat16"), ("X", 16400, "bfloat16"),
-        ("ONESB", 2048, "bfloat16"), ("ID", 128, "bfloat16"), ("IDN", 128, "bfloat16"), ("PK", 512, "bfloat16"),
-        ("HK", 512, "bfloat16"), ("TRI", 128, "bfloat16"), ("SEL", 1024, "bfloat16"), ("LA", 2048, "bfloat16"),
-        ("LB", 2048, "bfloat16"), ("LR", 2048, "bfloat16"), ("KI", 8, "int32"), ("KF", 32, "float32"), ("G1", 64, "float32"),
+        ("ONE1", 128, "bfloat16"), ("ONE2", 1024, "bfloat16"), ("FOUR", 8, "bfloat16"), ("GA", 8, "bfloat16"), ("GB", 8, "bfloat16"),
+        ("ID", 128, "bfloat16"), ("IDN", 128, "bfloat16"), ("PK", 512, "bfloat16"),
+        ("HK", 512, "bfloat16"), ("TRI", 128, "bfloat16"), ("SEL", 1024, "bfloat16"),
+        ("LR", 2048, "bfloat16"), ("KI", 8, "int32"), ("KF", 32, "float32"), ("G1", 64, "float32"),
         ("G2", 64, "float32"), ("G3", 64, "float32"), ("G4", 32, "float32"), ("G5", 32, "float32"), ("IC4", 4, "float32"),
         ("EM", 8, "float32"), ("EV", 8, "float32"), ("EI", 4, "int32"), ("W", 64, "bfloat16"), ("C4", 16, "bfloat16"),
         ("OFX", 32, "uint16"), ("OFF", 32, "uint16"), ("PT", 128, "int32"), ("ST", 32, "int32"), ("ST4", 32, "int32"),
         ("OFP", 128, "uint16"), ("QT", 128, "bfloat16"), ("CM", 2048, "bfloat16"), ("RES", 32, "float32"),
-        ("I0", 16, "int32"), ("J0", 32, "int32"), ("O0", 32, "uint16"), ("Z0", 256, "bfloat16"), ("Y0", 256, "bfloat16"), ("E0", 256, "bfloat16"),
-        ("I1", 16, "int32"), ("J1", 32, "int32"), ("O1", 32, "uint16"), ("Z1", 256, "bfloat16"), ("Y1", 256, "bfloat16"), ("E1", 256, "bfloat16")):
+        ("I0", 16, "int32"), ("J0", 32, "int32"), ("O0", 32, "uint16"), ("Z0", 256, "bfloat16"), ("YE0", 512, "bfloat16"), ("U0", 16, "float32"),
+        ("I1", 16, "int32"), ("J1", 32, "int32"), ("O1", 32, "uint16"), ("Z1", 256, "bfloat16"), ("YE1", 512, "bfloat16"), ("U1", 16, "float32")):
     SCRATCH[_n] = ("sbuf", [128, _w], _d)
 SEMAPHORES = (["vq", "aq", "pq", "gq", "dp", "ds", "dsp", "dss", "lpt", "lst", "rep", "yself", "yout",
                "arrP", "arrS", "arrX", "arrC", "arrF", "locP", "locS", "locX", "locC", "locF"] + ["b%d" % _i for _i in range(8)])
@@ -122,89 +123,78 @@ def rank_program(g, core, T, topo):
         dma("s" if s % 2 == 0 else "a", T.D32[:, 256 * s:256 * s + 256], T.bwt[s:s + 1, :], "b%d" % s, [], ["D32%d" % s])
     dma("s", T.PL[rank], T.pats[16 * rank:16 * rank + 16, :], "dsp", [], ["PLs"])
     dma("s", T.SL[rank], T.starts[16 * rank:16 * rank + 16, :], "dss", [], ["SLs"])
-    V("memset", (T.ONESB[:], 1.0), [], ["ONESB"])
-    op("g", "asel", (T.ID[:], T.ONESB[:, 0:128], [[-1, 128]], A.is_equal, 0.0, 0, 1), ["ONESB"], ["ID"])
-    for i in range(4):
-        V("ts", (T.PK[:, 128 * i:128 * i + 128], T.ID[:], float(4 ** i), None, A.mult), ["ID"], ["PK"])
-    send(lambda d: T.PP[d], T.PL[rank], "arrP", "locP", ["PP"])
-    send(lambda d: T.SS[d], T.SL[rank], "arrS", "locS", ["SS"])
-
-    CH = 5.0 * float(np.log(2.0))
-    for hh in range(2):
-        for s in range(4 * hh, 4 * hh + 4):
-            c0 = 256 * s
-            V("copy", (T.D[:, c0:c0 + 256], T.D32[:, c0:c0 + 256]), ["D32%d" % s], ["D%d" % s])
-            op("a", "act", (T.CE[:, c0:c0 + 256], T.D[:, c0:c0 + 256], AF.Exp), ["D%d" % s], ["CE%d" % s], scale=CH)
-        lo, hi = 1024 * hh, 1024 * hh + 1024
-        mms([(T.PSA[:, 512 * hh:512 * hh + 256], T.PK[:, 128 * i:128 * i + 128], T.D[:, lo + i:hi:4], i == 0, i == 3) for i in range(4)],
-            ["D%d" % s for s in range(4 * hh, 4 * hh + 4)] + ["PK"], ["A%d" % hh])
-        V("copy", (T.SENDX[:, 256 * hh:256 * hh + 256], T.PSA[:, 512 * hh:512 * hh + 256]), ["A%d" % hh], ["A%d" % hh, "SENDX%d" % hh])
-    send(lambda d: T.SENDX[:, 64 * d:64 * d + 64], T.LX[:, 64 * rank:64 * rank + 64], "arrX", "locX", ["SENDX0", "SENDX1"])
-    for hh in range(2):
-        lo, hi, o = 1024 * hh, 1024 * hh + 1024, 1024 + 512 * hh
-        mms([(T.PSA[:, o:o + 64], T.ID[:], T.CE[:, lo + q:hi:16], q == 0, q == 15) for q in range(16)],
-            ["CE%d" % s for s in range(4 * hh, 4 * hh + 4)] + ["ID"], ["A%d" % (2 + hh)])
-        V("copy", (T.SENDC[:, 64 * hh:64 * hh + 64], T.PSA[:, o:o + 64]), ["A%d" % (2 + hh)], ["A%d" % (2 + hh), "SENDC%d" % hh])
-    send(lambda d: T.SENDC[:, 16 * d:16 * d + 16], T.LC[:, 16 * rank:16 * rank + 16], "arrC", "locC", ["SENDC0", "SENDC1"])
-    h = rank // 4
-    V("copy", (T.LX[:, 64 * rank:64 * rank + 64], T.SENDX[:, 64 * rank:64 * rank + 64]), ["SENDX%d" % h], ["LXs"])
-    V("copy", (T.LC[:, 16 * rank:16 * rank + 16], T.SENDC[:, 16 * rank:16 * rank + 16]), ["SENDC%d" % h], ["LCs"])
 
     fl = dict(allow_small_or_imprecise_dtypes=True)
+    V("memset", (T.ONE1[:], 1.0), [], ["ONE1"])
     op("g", "iota", (T.KI[:, 0:1], [[0, 1]], 0, 1), [], ["KI0"])
+    op("g", "asel", (T.ID[:], T.ONE1[:], [[-1, 128]], A.is_equal, 0.0, 0, 1), ["ONE1"], ["ID"])
     op("g", "iota", (T.G4[:], [[4, 16], [256, 2]], 0, 0), [], ["G4"], **fl)
     op("g", "iota", (T.G5[:], [[1, 16], [64, 2]], 0, 0), [], ["G5"], **fl)
     op("g", "iota", (T.G1[:], [[1, 16], [0, 4]], 0, 0), [], ["G1"], **fl)
     op("g", "iota", (T.G2[:], [[0, 16], [32, 4]], 6144, 0), [], ["G2"], **fl)
     op("g", "iota", (T.IC4[:], [[1, 4]], 0, 0), [], ["IC4"], **fl)
-    op("g", "asel", (T.TRI[:], T.ONESB[:, 0:128], [[1, 128]], A.is_ge, 0.0, -1, -1), ["ONESB"], ["TRI"])
-    op("g", "asel", (T.SEL[:], T.ONESB[:, 0:1024], [[-16, 8], [0, 8], [-1, 16]], A.is_equal, 0.0, 0, 1), ["ONESB"], ["SEL"])
-    op("g", "asel", (T.LA[:], T.ONESB[:], [[-1, 16], [0, 8], [1, 16]], A.is_equal, 0.0, 0, 0), ["ONESB"], ["LA"])
-    op("g", "asel", (T.LB[:], T.LA[:], [[0, 16], [-16, 8], [0, 16]], A.is_ge, 0.0, 0, 1), ["LA"], ["LB"])
-    op("g", "asel", (T.LR[:], T.LB[:], [[0, 16], [16, 8], [0, 16]], A.is_ge, 0.0, 15, -1), ["LB"], ["LR"])
+    send(lambda d: T.PP[d], T.PL[rank], "arrP", "locP", ["PP"])
+    send(lambda d: T.SS[d], T.SL[rank], "arrS", "locS", ["SS"])
     for d, n, sh in ((1, 15, 0), (2, 3, 0), (3, 3, 2), (4, 1, 0), (5, 1, 1)):
         V("ts", (T.KI[:, d:d + 1], T.KI[:, 0:1], sh, n, A.arith_shift_right, A.bitwise_and), ["KI0"], ["KI"])
     V("copy", (T.KF[:, 0:6], T.KI[:, 0:6]), ["KI", "KI0"], ["KF"])
     col = lambda j: T.KF[:, j:j + 1]
-    V("ts", (col(19), col(3), 64.0, None, A.mult), ["KF"], ["K19"])
-    V("tt", (col(20), col(19), col(2), A.add), ["K19", "KF"], ["K20"])
-    V("ts", (T.OFX[:], T.G4[:], col(20), None, A.add), ["G4", "K20"], ["OFX"])
-    V("ts", (col(13), col(4), -5120.0, 20480.0, A.mult, A.add), ["KF"], ["K13"])
+    for i in range(4):
+        V("ts", (T.PK[:, 128 * i:128 * i + 128], T.ID[:], float(4 ** i), None, A.mult), ["ID"], ["PK"])
+    for j, src, k1, k2 in ((19, 3, 64.0, 0.0), (13, 4, -5120.0, 20480.0), (16, 5, -5120.0, 0.0), (6, 4, 31.0, 1.0), (7, 5, 1023.0, 1.0),
+                           (9, 4, -31.0 / 32, 1.0), (10, 5, -1023.0 / 1024, 1.0), (21, 2, 128.0, 0.0), (22, 3, 16.0, 0.0)):
+        V("ts", (col(j), col(src), k1, k2, A.mult, A.add), ["KF"], ["K%d" % j])
     V("tt", (col(14), col(4), col(5), A.mult), ["KF"], ["K14"])
-    V("ts", (col(15), col(14), -15360.0, None, A.mult), ["K14"], ["K15"])
-    V("ts", (col(16), col(5), -5120.0, None, A.mult), ["KF"], ["K16"])
-    V("tt", (col(17), col(13), col(15), A.add), ["K13", "K15"], ["K17"])
-    V("tt", (col(18), col(17), col(16), A.add), ["K17", "K16"], ["K18"])
-    V("ts", (col(6), col(4), 31.0, 1.0, A.mult, A.add), ["KF"], ["K6"])
-    V("ts", (col(7), col(5), 1023.0, 1.0, A.mult, A.add), ["KF"], ["K7"])
     V("tt", (col(8), col(6), col(7), A.mult), ["K6", "K7"], ["K8"])
-    V("ts", (col(9), col(4), -31.0 / 32, 1.0, A.mult, A.add), ["KF"], ["K9"])
-    V("ts", (col(10), col(5), -1023.0 / 1024, 1.0, A.mult, A.add), ["KF"], ["K10"])
     V("tt", (col(11), col(9), col(10), A.mult), ["K9", "K10"], ["K11"])
-    V("ts", (col(12), col(11), 0.5, -0.5, A.mult, A.add), ["K11"], ["K12"])
-    V("ts", (col(21), col(2), 128.0, None, A.mult), ["KF"], ["K21"])
-    V("ts", (col(22), col(3), 16.0, None, A.mult), ["KF"], ["K22"])
+    V("tt", (col(20), col(19), col(2), A.add), ["K19", "KF"], ["K20"])
     V("tt", (col(23), col(21), col(22), A.add), ["K21", "K22"], ["K23"])
-    V("ts", (T.OFF[:], T.G5[:], col(23), None, A.add), ["G5", "K23"], ["OFF"])
-    V("ts", (T.G3[:], T.G1[:], col(1), None, A.is_gt), ["G1", "KF"], ["G3"])
-    V("tt", (T.W[:], T.G3[:], T.G2[:], A.mult), ["G3", "G2"], ["W"])
-    V("ts", (T.C4[:, 0:4], T.IC4[:], col(3), col(8), A.is_equal, A.mult), ["IC4", "KF", "K8"], ["C4"])
-    V("ts", (T.EM[:, 0:4], T.IC4[:], col(3), None, A.is_equal), ["IC4", "KF"], ["EM"])
+    V("ts", (col(15), col(14), -15360.0 - 192.0, None, A.mult), ["K14"], ["K15"])
+    V("tt", (col(17), col(13), col(16), A.add), ["K13", "K16"], ["K17"])
+    V("ts", (col(12), col(11), 0.5, -0.5, A.mult, A.add), ["K11"], ["K12"])
+    V("tt", (col(18), col(17), col(15), A.add), ["K17", "K15"], ["K18"])
+    V("ts", (T.OFX[:], T.G4[:], col(20), None, A.add), ["G4", "K20"], ["OFX"])
+
+    CH = 5.0 * float(np.log(2.0))
+    for s in range(8):
+        c0 = 256 * s
+        V("copy", (T.D[:, c0:c0 + 256], T.D32[:, c0:c0 + 256]), ["D32%d" % s], ["D%d" % s])
+        op("a", "act", (T.CE[:, c0:c0 + 256], T.D[:, c0:c0 + 256], AF.Exp), ["D%d" % s], ["CE%d" % s], scale=CH)
+    for f in range(4):
+        lo, hi = 512 * f, 512 * f + 512
+        mms([(T.PSA[:, lo:lo + 128], T.PK[:, 128 * i:128 * i + 128], T.D[:, lo + i:hi:4], i == 0, i == 3) for i in range(4)],
+            ["D%d" % (2 * f), "D%d" % (2 * f + 1), "PK"], ["A%d" % f])
+        V("copy", (T.SENDX[:, 128 * f:128 * f + 128], T.PSA[:, lo:lo + 128]), ["A%d" % f], ["A%d" % f, "SENDX%d" % f])
+    send(lambda d: T.SENDX[:, 64 * d:64 * d + 64], T.LX[:, 64 * rank:64 * rank + 64], "arrX", "locX", ["SENDX%d" % f for f in range(4)])
+    for hh in range(2):
+        lo, hi, o = 1024 * hh, 1024 * hh + 1024, 512 * hh
+        mms([(T.PSB[:, o:o + 64], T.ID[:], T.CE[:, lo + q:hi:16], q == 0, q == 15) for q in range(16)],
+            ["CE%d" % s for s in range(4 * hh, 4 * hh + 4)] + ["ID"], ["B%d" % hh])
+        V("copy", (T.SENDC[:, 64 * hh:64 * hh + 64], T.PSB[:, o:o + 64]), ["B%d" % hh], ["B%d" % hh, "SENDC%d" % hh])
+    send(lambda d: T.SENDC[:, 16 * d:16 * d + 16], T.LC[:, 16 * rank:16 * rank + 16], "arrC", "locC", ["SENDC0", "SENDC1"])
+    V("copy", (T.LX[:, 64 * rank:64 * rank + 64], T.SENDX[:, 64 * rank:64 * rank + 64]), ["SENDX%d" % (rank // 2)], ["LXs"])
+    V("copy", (T.LC[:, 16 * rank:16 * rank + 16], T.SENDC[:, 16 * rank:16 * rank + 16]), ["SENDC%d" % (rank // 4)], ["LCs"])
+
+    for i, k in enumerate((-1.0, -28.0, -896.0, 4096.0)):
+        V("ts", (T.HK[:, 128 * i:128 * i + 128], T.ID[:], k, None, A.mult), ["ID"], ["HK"])
+    V("memset", (T.ONE2[:], 1.0), [], ["ONE2"])
+    V("memset", (T.FOUR[:], 4.0), [], ["FOUR"])
     V("memset", (T.MK[:], 1.0), [], ["MK0"])
-    V("memset", (T.MK[:, 0:512:16], 0.0), ["MK0"], ["MK"])
     V("memset", (T.ONE32[:], 1.0), [], ["ONE32"])
     V("memset", (T.BASE[:, 0:1], 0.0), [], ["BASE0"])
     V("memset", (T.TB[:, 3:2048:4], 0.0), [], ["TB3"])
+    V("memset", (T.MK[:, 0:512:16], 0.0), ["MK0"], ["MK"])
     V("ts", (T.IDN[:], T.ID[:], -1.0, None, A.mult), ["ID"], ["IDN"])
-    for i, k in enumerate((-1.0, -28.0, -896.0, 4096.0)):
-        V("ts", (T.HK[:, 128 * i:128 * i + 128], T.ID[:], k, None, A.mult), ["ID"], ["HK"])
+    V("ts", (T.OFF[:], T.G5[:], col(23), None, A.add), ["G5", "K23"], ["OFF"])
+    V("ts", (T.C4[:, 0:4], T.IC4[:], col(3), col(8), A.is_equal, A.mult), ["IC4", "KF", "K8"], ["C4"])
+    V("memset", (T.LR[:], 0.0), [], ["LR"])
+    op("g", "asel", (T.TRI[:], T.ONE1[:], [[1, 128]], A.is_ge, 0.0, -1, -1), ["ONE1"], ["TRI"])
+    op("g", "asel", (T.SEL[:], T.ONE2[:], [[-16, 8], [0, 8], [-1, 16]], A.is_equal, 0.0, 0, 1), ["ONE2"], ["SEL"])
+    op("g", "asel", (T.GA[:], T.FOUR[:], [[-16, 8]], A.is_ge, 0.0, 0, 1), ["FOUR"], ["GA"])
+    op("g", "asel", (T.GB[:], T.GA[:], [[16, 8]], A.is_ge, 0.0, 15, -1), ["GA"], ["GB"])
     dma("s", T.PT[:], T.PL[:], "lpt", ["PL", "PLs"], ["PT"])
     dma("s", T.ST[:], T.SL[:], "lst", ["SL", "SLs"], ["ST"])
     V("copy", (T.OFP[:], T.PT[:]), ["PT"], ["OFP"])
-    V("ts", (T.QT[:], T.PT[:], 0.25, None, A.mult), ["PT"], ["QT"])
-    V("ts", (T.ST4[:], T.ST[:], 4.0, None, A.mult), ["ST"], ["ST4"])
-    for h in range(2):
-        V("tt", (T["I%d" % h][:], T.ST4[:, 16 * h:16 * h + 16], T.PT[:, 0:16], A.add), ["ST4", "PT"], ["I%d" % h])
 
     TAK, TBK = ["TA0", "TA1", "TA2", "TA3"], ["TB0", "TB1", "TB2", "TB3"]
     op("a", "act", (T.LXP[:], T.LX[:, 0:512].indirect(T.OFX[:, 0:32]), AF.Copy), ["LX", "LXs", "OFX"], ["LXP"])
@@ -215,15 +205,7 @@ def rank_program(g, core, T, topo):
     for i in range(3):
         sc = 32.0 / 4 ** i
         op("a", "act", (T.TB[:, i:2048:4], T.LXP[:], AF.Copy), ["LXP"], ["TB%d" % i], scale=sc, bias=sc * B_T[i + 1])
-    op("a", "act", (T.HNS[:], T.PSB[:, 0:512], AF.Copy), ["B0"], ["B0", "HNS"])
-    for bk in range(4):
-        cs = []
-        for il in range(4 * bk, 4 * bk + 4):
-            o = T.PSA[:, 128 * il:128 * il + 128]
-            cs += [(o, T.TA[:, 128 * il:128 * il + 128], T.ID[:], True, False), (o, T.TB[:, 128 * il:128 * il + 128], T.IDN[:], False, True)]
-        mms(cs, TAK + TBK + ["ID", "IDN"], ["A%d" % bk])
-        op("a", "act", (T.XL[:, 512 * bk:512 * bk + 512], T.PSA[:, 512 * bk:512 * bk + 512], AF.Identity), ["A%d" % bk, "K18"],
-           ["A%d" % bk, "XL%d" % bk], bias=col(18))
+    op("a", "act", (T.HNS[:], T.PSB[:, 0:512], AF.Identity), ["B0"], ["B0", "HNS"], bias=float(BIAS - 16240640))
     op("a", "act", (T.CM[:], T.C4[:, 0:4].indirect(T.OFP[:, 0:128]), AF.Copy), ["C4", "OFP"], ["CM"])
 
     V("copy", (T.CI[:], T.LC[:]), ["LC", "LCs"], ["CI"])
@@ -233,33 +215,51 @@ def rank_program(g, core, T, topo):
     V("copy", (T.N15[:], T.CX[:, 15:512:16]), ["CX"], ["N15"])
     V("memset", (T.NS[:, 0:512:16], 0.0), ["NS"], ["NS"])
     V("scan", (T.S1[:], T.MK[:], T.NS[:], 0.0, A.mult, A.add), ["MK", "NS"], ["S1"])
-    for j, (m, k) in enumerate(((T.ONESB[:, 0:128], "ONESB"), (T.TRI[:], "TRI"))):
+    for j, (m, k) in enumerate(((T.ONE1[:], "ONE1"), (T.TRI[:], "TRI"))):
         o = T.PSB[:, 512 + 512 * j:544 + 512 * j]
         mms([(o, m, T.S1[:, 15:512:16], True, False), (o, m, T.N15[:], False, True)], ["S1", "N15", k], ["B%d" % (1 + j)])
     V("scan", (T.BASE[:, 1:33], T.ONE32[:], T.PSB[:, 512:544], 0.0, A.mult, A.add), ["B1", "ONE32"], ["B1", "BASE"])
     V("tt", (T.NS[:, 0:512:16], T.PSB[:, 1024:1056], T.BASE[:, 0:32], A.add), ["B2", "BASE", "BASE0"], ["B2", "NS"])
     V("scan", (T.F[:], T.MK[:], T.NS[:], 0.0, A.mult, A.add), ["MK", "NS"], ["F"])
     V("tt", (T.NI[:], T.F[:, 0:512].indirect(T.OFF[:, 0:32]), T.HNS[:], A.add), ["F", "OFF", "HNS"], ["NI"])
-    for i in range(4):
-        V("ts", (T.DI[:, 512 * i:512 * i + 512], T.NI[:], 5 * i, 15 if i == 3 else 31, A.arith_shift_right, A.bitwise_and), ["NI"], ["DI%d" % i])
-    for i in range(4):
-        V("copy", (T.DB[:, i:2048:4], T.DI[:, 512 * i:512 * i + 512]), ["DI%d" % i], ["DB%d" % i])
+
     for bk in range(4):
-        mms([(T.PSA[:, 128 * il:128 * il + 128], T.DB[:, 128 * il:128 * il + 128], T.ID[:], True, True) for il in range(4 * bk, 4 * bk + 4)],
-            ["DB0", "DB1", "DB2", "DB3", "ID"], ["A%d" % bk])
+        cs = []
         for il in range(4 * bk, 4 * bk + 4):
-            V("tt", (T.XC[:, il:2048:16], T.PSA[:, 128 * il:128 * il + 128], T.XL[:, 128 * il:128 * il + 128], A.add),
-              ["A%d" % bk, "XL%d" % bk], ["A%d" % bk, "XC"])
-    XK = ["XE"]
+            o = T.PSA[:, 128 * il:128 * il + 128]
+            cs += [(o, T.TA[:, 128 * il:128 * il + 128], T.ID[:], True, False), (o, T.TB[:, 128 * il:128 * il + 128], T.IDN[:], False, True)]
+        mms(cs, TAK + TBK + ["ID", "IDN"], ["A%d" % bk])
+        op("a", "act", (T.XL[:, 512 * bk:512 * bk + 512], T.PSA[:, 512 * bk:512 * bk + 512], AF.Identity), ["A%d" % bk, "K18"],
+           ["A%d" % bk, "XL%d" % bk], bias=col(18))
+    for bk in range(2):
+        mms([(T.PSA[:, 512 * bk:512 * bk + 512], T.ID[:], T.XL[:, 512 * bk:512 * bk + 512], True, False)], ["XL%d" % bk, "ID"], ["A%d" % bk])
+    XCK = ["XC%d" % bk for bk in range(4)]
+    for e in range(2):
+        n0, n1, m0, m1 = 256 * e, 256 * e + 256, 1024 * e, 1024 * e + 1024
+        V("ts", (T.DB[:, m0 + 3:m1:4], T.NI[:, n0:n1], 2.0 ** -15, 191.5 + 2.0 ** -16, A.mult, A.add), ["NI"], ["DB3%d" % e])
+        for i in range(3):
+            V("ts", (T.DI[:, 512 * i + n0:512 * i + n1], T.NI[:, n0:n1], 5 * i, 31, A.arith_shift_right, A.bitwise_and), ["NI"], ["DI%d%d" % (i, e)])
+        for i in range(3):
+            V("copy", (T.DB[:, m0 + i:m1:4], T.DI[:, 512 * i + n0:512 * i + n1]), ["DI%d%d" % (i, e)], ["DB%d%d" % (i, e)])
+        for bk in (2 * e, 2 * e + 1):
+            mms([(T.PSA[:, 128 * il:128 * il + 128], T.DB[:, 128 * il:128 * il + 128], T.ID[:], e == 1, e == 1 or il % 4 == 3) for il in range(4 * bk, 4 * bk + 4)],
+                ["DB%d%d" % (i, e) for i in (3, 0, 1, 2)] + ["ID"], ["A%d" % bk])
+            for il in range(4 * bk, 4 * bk + 4):
+                o, x = T.XC[:, il:2048:16], T.PSA[:, 128 * il:128 * il + 128]
+                if e == 1:
+                    V("tt", (o, x, T.XL[:, 128 * il:128 * il + 128], A.add), ["A%d" % bk, "XL%d" % bk], ["A%d" % bk, XCK[bk]])
+                else:
+                    op("a", "act", (o, x, AF.Copy), ["A%d" % bk], ["A%d" % bk, XCK[bk]])
+    XK, LK = ["XE"], ["LR%d" % y for y in range(8)]
     for k in range(NPE, 8):
         for y in range(8):
-            dma("s", T.X[16 * y:16 * y + 16, 2048 * k:2048 * k + 2048], T.XC[16 * k:16 * k + 16, :], "rep", ["XC"], ["XD%d%d" % (k, y)])
+            dma("s", T.X[16 * y:16 * y + 16, 2048 * k:2048 * k + 2048], T.XC[16 * k:16 * k + 16, :], "rep", XCK, ["XD%d%d" % (k, y)])
             XK.append("XD%d%d" % (k, y))
     n = 0
     for k in range(NPE):
         for j in range(4):
             b = n % 4
-            mms([(T.PSB[:, 512 * b:512 * b + 512], T.SEL[:, 128 * k:128 * k + 128], T.XC[:, 512 * j:512 * j + 512], True, True)], ["XC", "SEL"], ["B%d" % b])
+            mms([(T.PSB[:, 512 * b:512 * b + 512], T.SEL[:, 128 * k:128 * k + 128], T.XC[:, 512 * j:512 * j + 512], True, True)], XCK + ["SEL"], ["B%d" % b])
             o, x = T.X[:, 2048 * k + 512 * j:2048 * k + 512 * j + 512], T.PSB[:, 512 * b:512 * b + 512]
             if n % 2 == 0:
                 V("copy", (o, x), ["B%d" % b], ["B%d" % b, "X%d" % n])
@@ -267,38 +267,61 @@ def rank_program(g, core, T, topo):
                 op("a", "act", (o, x, AF.Copy), ["B%d" % b], ["B%d" % b, "X%d" % n])
             XK.append("X%d" % n)
             n += 1
-    V("tt", (T.EV[:, 0:4], T.EM[:, 0:4], T.BASE[:, 8:33:8], A.mult), ["EM", "BASE"], ["EV"])
-    V("red", (T.EV[:, 4:5], T.EV[:, 0:4], AxisListType.X, A.add), ["EV"], ["EV4"])
-    V("ts", (T.EV[:, 5:6], T.EV[:, 4:5], 512000.0, col(11), A.add, A.mult), ["EV4", "K11"], ["EV5"])
-    V("ts", (T.EI[:, 0:1], T.EV[:, 5:6], col(12), None, A.add), ["EV5", "K12"], ["EI0"])
-    V("ts", (T.EI[:, 1:2], T.EI[:, 0:1], 31, None, A.bitwise_and), ["EI0"], ["EI1"])
-    V("copy", (T.X[:, 16384:16385], T.EI[:, 1:2]), ["EI1"], ["XE"])
+            if n == 2:
+                V("ts", (T.G3[:], T.G1[:], col(1), None, A.is_gt), ["G1", "KF"], ["G3"])
+                V("ts", (T.QT[:], T.PT[:], 1.0, None, A.mult), ["PT"], ["QT"])
+                V("ts", (T.ST4[:], T.ST[:], 4.0, None, A.mult), ["ST"], ["ST4"])
+                V("ts", (T.EM[:, 0:4], T.IC4[:], col(3), None, A.is_equal), ["IC4", "KF"], ["EM"])
+                V("tt", (T.EV[:, 0:4], T.EM[:, 0:4], T.BASE[:, 8:33:8], A.mult), ["EM", "BASE"], ["EV"])
+            if n == 4:
+                V("tt", (T.W[:], T.G3[:], T.G2[:], A.mult), ["G3", "G2"], ["W"])
+                for h in range(2):
+                    V("tt", (T["I%d" % h][:], T.ST4[:, 16 * h:16 * h + 16], T.PT[:, 0:16], A.add), ["ST4", "PT"], ["I%d" % h])
+                V("red", (T.EV[:, 4:5], T.EV[:, 0:4], AxisListType.X, A.add), ["EV"], ["EV4"])
+            if n in (6, 8):
+                for y in range(2 * n - 12, 2 * n - 8):
+                    V("ts", (T.LR[:, 16 * y:16 * y + 1936:129], T.ONE1[:, 0:16], T.GB[:, y:y + 1], None, A.mult), ["ONE1", "GB", "LR"], [LK[y]])
+            if n == 6:
+                V("ts", (T.EV[:, 5:6], T.EV[:, 4:5], float(BIAS), col(11), A.add, A.mult), ["EV4", "K11"], ["EV5"])
+            if n == 8:
+                V("ts", (T.EI[:, 0:1], T.EV[:, 5:6], col(12), None, A.add), ["EV5", "K12"], ["EI0"])
+            if n == 10:
+                V("ts", (T.EI[:, 1:2], T.EI[:, 0:1], 31, None, A.bitwise_and), ["EI0"], ["EI1"])
+            if n == 12:
+                V("copy", (T.X[:, 16384:16385], T.EI[:, 1:2]), ["EI1"], ["XE"])
 
-    for t in range(8):
-        for h in range(2):
-            s = str(h)
-            I, J, O, Z, Y, E = (T[x + s] for x in "IJOZYE")
-            ps, pk = T.PSA[:, 512 * h:512 * h + 16], "A" + s
-            if t:
-                V("ts", (I[:], ps, 4.0, OFFS, A.mult, A.add), [pk], [pk, "I" + s])
+    def small(n):
+        t, h = n // 2, n % 2
+        s = str(h)
+        I, J, O = T["I" + s], T["J" + s], T["O" + s]
+        ps, pk = 512 * h, "A" + s
+        if n >= 2:
+            op("a", "act", (T["U" + s][:], T.PSA[:, ps:ps + 16], AF.Identity), [pk], [pk, "U" + s], bias=-4.0 * BIAS)
+            V("tt", (I[:], T.PSA[:, ps + 16:ps + 32], T["U" + s][:], A.add), [pk, "U" + s], [pk, "I" + s])
+        if t < 8:
             V("ts", (J[:, 0:16], I[:], 6, 0x7FFF, A.arith_shift_right, A.bitwise_and), ["I" + s], ["J" + s])
             V("ts", (J[:, 16:32], I[:], 63, None, A.bitwise_and), ["I" + s], ["J" + s])
             V("copy", (O[:], J[:]), ["J" + s], ["O" + s])
-            xb = T.X[:, 0:16385].indirect(O[:, 0:16])
-            op("a", "act", (Z[:], xb, AF.Identity), ["O" + s] + XK, ["Z" + s], bias=6128.5)
-            V("tt", (Y[:], xb, T.CM[:, 256 * t:256 * t + 256], A.mult), ["O" + s, "CM"] + XK, ["Y" + s])
-            V("tt", (E[:], T.W[:, 0:64].indirect(O[:, 16:32]), Z[:], A.is_equal), ["O" + s, "W", "Z" + s], ["E" + s])
-            cs = [(ps, T.LR[:, 128 * r:128 * r + 128], Y[:, r:256:16], r == 0, False) for r in range(16)]
-            if t < 7:
-                cs.append((ps, T.ID[:], T.QT[:, 16 * t + 16:16 * t + 32], False, False))
-            mms(cs, ["Y" + s, "LR", "QT", "ID"], [pk])
-            mms([(ps, T.LR[:, 128 * r:128 * r + 128], E[:, r:256:16], False, r == 15) for r in range(16)], ["E" + s, "LR"], [pk])
-    for h in range(2):
+            op("a", "act", (T["Z" + s][:], T.X[:, 0:16385].indirect(O[:, 0:16]), AF.Identity), ["O" + s] + XK, ["Z" + s], bias=6128.5)
+        else:
+            V("ts", (J[:, 0:16], I[:], 2, 0x7FFFF, A.arith_shift_right, A.bitwise_and), ["I" + s], ["J" + s])
+            V("copy", (T.RES[:, 16 * h:16 * h + 16], J[:, 0:16]), ["J" + s], ["RES%d" % h])
+
+    def big(n):
+        t, h = n // 2, n % 2
         s = str(h)
-        ps, pk = T.PSA[:, 512 * h:512 * h + 16], "A" + s
-        V("ts", (T["I" + s][:], ps, 4.0, OFFS, A.mult, A.add), [pk], [pk, "I" + s])
-        V("ts", (T["J" + s][:, 0:16], T["I" + s][:], 2, 0x7FFFF, A.arith_shift_right, A.bitwise_and), ["I" + s], ["J" + s])
-        V("copy", (T.RES[:, 16 * h:16 * h + 16], T["J" + s][:, 0:16]), ["J" + s], ["RES%d" % h])
+        O, YE, ps = T["O" + s], T["YE" + s], 512 * h
+        V("tt", (YE[:, 0:256], T.X[:, 0:16385].indirect(O[:, 0:16]), T.CM[:, 256 * t:256 * t + 256], A.mult), ["O" + s, "CM"] + XK, ["Y" + s])
+        V("tt", (YE[:, 256:512], T.W[:, 0:64].indirect(O[:, 16:32]), T["Z" + s][:], A.is_equal), ["O" + s, "W", "Z" + s], ["E" + s])
+        cs = [(T.PSA[:, ps:ps + 32], T.LR[:, 128 * r:128 * r + 128], YE[:, r:512:16], r == 0, r == 15) for r in range(16)]
+        if t < 7:
+            cs.insert(1, (T.PSA[:, ps:ps + 16], T.ID[:], T.QT[:, 16 * t + 16:16 * t + 32], False, False))
+        mms(cs, ["Y" + s, "E" + s, "QT", "ID"] + LK, ["A" + s])
+
+    for n in range(18):
+        if 0 < n < 17:
+            big(n - 1)
+        small(n)
     send(lambda d: T.RES[:], T.FL[rank], "arrF", "locF", ["RES0", "RES1"])
     r0, r1 = 16 * rank, 16 * rank + 16
     dma("s", T.y[r0:r1, :], T.RES[r0:r1, :], "yself", ["RES0", "RES1"], ["y0"])

@@ -2,14 +2,16 @@ import numpy as np
 from concourse.bass import DstId, RemoteDMATransfer
 from concourse.mybir import AluOpType as A, AxisListType, ActivationFunctionType as AF
 
-NPE = 5
-BIAS = 131072
+NPE = 4
+BIAS = 507904
+BIG = 2097152
+RND = 402653184.0
 B_T = (0.0, 638.5, 2552.5, 10208.5)
 
 SCRATCH = {
     "PP": ("dram", [8, 128, 16], "int32"), "SS": ("dram", [8, 128, 4], "int32"),
     "PL": ("dram", [8, 128, 16], "int32"), "SL": ("dram", [8, 128, 4], "int32"),
-    "FL": ("dram", [8, 128, 32], "float32"),
+    "RD": ("dram", [8, 128, 4], "float32"), "FL": ("dram", [8, 128, 4], "float32"),
     "PSA": ("psum", [128, 2048], "float32"), "PSB": ("psum", [128, 2048], "float32"),
 }
 for _n, _w, _d in (
@@ -19,18 +21,22 @@ for _n, _w, _d in (
         ("S1", 512, "bfloat16"), ("N15", 32, "bfloat16"), ("MK", 512, "float32"), ("BASE", 40, "float32"),
         ("ONE32", 32, "float32"), ("F", 512, "float32"), ("HNS", 512, "float32"), ("NI", 512, "int32"), ("DI", 2048, "int32"),
         ("DB", 2048, "bfloat16"), ("XL", 2048, "bfloat16"), ("XC", 2048, "bfloat16"), ("X", 16400, "bfloat16"),
-        ("ONE1", 128, "bfloat16"), ("ONE2", 1024, "bfloat16"), ("FOUR", 8, "bfloat16"), ("GA", 8, "bfloat16"), ("GB", 8, "bfloat16"),
+        ("ONE1", 128, "bfloat16"), ("ONE2", 1024, "bfloat16"), ("FOUR", 32, "bfloat16"), ("GA", 32, "bfloat16"), ("GB", 32, "bfloat16"),
         ("ID", 128, "bfloat16"), ("IDN", 128, "bfloat16"), ("PK", 512, "bfloat16"),
         ("HK", 512, "bfloat16"), ("TRI", 128, "bfloat16"), ("SEL", 1024, "bfloat16"),
-        ("LR", 2048, "bfloat16"), ("KI", 8, "int32"), ("KF", 32, "float32"), ("G1", 64, "float32"),
+        ("SELY", 32, "bfloat16"), ("SELZ", 32, "bfloat16"), ("SELL", 16, "bfloat16"),
+        ("KI", 8, "int32"), ("KF", 32, "float32"), ("G1", 64, "float32"),
         ("G2", 64, "float32"), ("G3", 64, "float32"), ("G4", 32, "float32"), ("G5", 32, "float32"), ("IC4", 4, "float32"),
-        ("EM", 8, "float32"), ("EV", 8, "float32"), ("EI", 4, "int32"), ("W", 64, "bfloat16"), ("C4", 16, "bfloat16"),
+        ("EM", 8, "float32"), ("EV", 8, "float32"), ("EI", 4, "int32"), ("WF", 64, "float32"), ("W", 64, "bfloat16"), ("LW", 16, "bfloat16"),
         ("OFX", 32, "uint16"), ("OFF", 32, "uint16"), ("PT", 128, "int32"), ("ST", 32, "int32"), ("ST4", 32, "int32"),
-        ("OFP", 128, "uint16"), ("QT", 128, "bfloat16"), ("CM", 2048, "bfloat16"), ("RES", 32, "float32"),
-        ("I0", 16, "int32"), ("J0", 32, "int32"), ("O0", 32, "uint16"), ("Z0", 256, "bfloat16"), ("YE0", 512, "bfloat16"), ("U0", 16, "float32"),
-        ("I1", 16, "int32"), ("J1", 32, "int32"), ("O1", 32, "uint16"), ("Z1", 256, "bfloat16"), ("YE1", 512, "bfloat16"), ("U1", 16, "float32")):
+        ("OFP", 128, "uint16"), ("PTB", 128, "bfloat16"), ("LTR", 2048, "bfloat16"), ("AM", 512, "bfloat16"), ("QTB", 512, "bfloat16"),
+        ("RST", 64, "float32"), ("RES", 32, "float32"),
+        ("I0", 16, "int32"), ("J0", 16, "int32"), ("OA0", 16, "uint16"), ("OB0", 16, "uint16"), ("S0", 64, "float32"),
+        ("Z0", 256, "bfloat16"), ("ZL0", 256, "bfloat16"), ("E0", 256, "bfloat16"),
+        ("I1", 16, "int32"), ("J1", 16, "int32"), ("OA1", 16, "uint16"), ("OB1", 16, "uint16"), ("S1B", 64, "float32"),
+        ("Z1", 256, "bfloat16"), ("ZL1", 256, "bfloat16"), ("E1", 256, "bfloat16")):
     SCRATCH[_n] = ("sbuf", [128, _w], _d)
-SEMAPHORES = (["vq", "aq", "pq", "gq", "dp", "ds", "dsp", "dss", "lpt", "lst", "rep", "yself", "yout",
+SEMAPHORES = (["vq", "aq", "pq", "gq", "dp", "ds", "dsp", "dss", "lpt", "lst", "rep", "yself", "yout", "rd",
                "arrP", "arrS", "arrX", "arrC", "arrF", "locP", "locS", "locX", "locC", "locF"] + ["b%d" % _i for _i in range(8)])
 
 
@@ -126,12 +132,13 @@ def rank_program(g, core, T, topo):
 
     fl = dict(allow_small_or_imprecise_dtypes=True)
     V("memset", (T.ONE1[:], 1.0), [], ["ONE1"])
+    V("memset", (T.FOUR[:], 4.0), [], ["FOUR"])
     op("g", "iota", (T.KI[:, 0:1], [[0, 1]], 0, 1), [], ["KI0"])
     op("g", "asel", (T.ID[:], T.ONE1[:], [[-1, 128]], A.is_equal, 0.0, 0, 1), ["ONE1"], ["ID"])
     op("g", "iota", (T.G4[:], [[4, 16], [256, 2]], 0, 0), [], ["G4"], **fl)
     op("g", "iota", (T.G5[:], [[1, 16], [64, 2]], 0, 0), [], ["G5"], **fl)
     op("g", "iota", (T.G1[:], [[1, 16], [0, 4]], 0, 0), [], ["G1"], **fl)
-    op("g", "iota", (T.G2[:], [[0, 16], [32, 4]], 6144, 0), [], ["G2"], **fl)
+    op("g", "iota", (T.G2[:], [[0, 16], [32, 4]], 1, 0), [], ["G2"], **fl)
     op("g", "iota", (T.IC4[:], [[1, 4]], 0, 0), [], ["IC4"], **fl)
     send(lambda d: T.PP[d], T.PL[rank], "arrP", "locP", ["PP"])
     send(lambda d: T.SS[d], T.SL[rank], "arrS", "locS", ["SS"])
@@ -139,19 +146,21 @@ def rank_program(g, core, T, topo):
         V("ts", (T.KI[:, d:d + 1], T.KI[:, 0:1], sh, n, A.arith_shift_right, A.bitwise_and), ["KI0"], ["KI"])
     V("copy", (T.KF[:, 0:6], T.KI[:, 0:6]), ["KI", "KI0"], ["KF"])
     col = lambda j: T.KF[:, j:j + 1]
+    op("a", "act", (col(8), col(2), AF.Exp), ["KF"], ["K8"], scale=float(np.log(32.0)))
     for i in range(4):
         V("ts", (T.PK[:, 128 * i:128 * i + 128], T.ID[:], float(4 ** i), None, A.mult), ["ID"], ["PK"])
-    for j, src, k1, k2 in ((19, 3, 64.0, 0.0), (13, 4, -5120.0, 20480.0), (16, 5, -5120.0, 0.0), (6, 4, 31.0, 1.0), (7, 5, 1023.0, 1.0),
+    for j, src, k1, k2 in ((19, 3, 64.0, 0.0), (13, 4, -5120.0, 20480.0), (16, 5, -5120.0, 0.0),
                            (9, 4, -31.0 / 32, 1.0), (10, 5, -1023.0 / 1024, 1.0), (21, 2, 128.0, 0.0), (22, 3, 16.0, 0.0)):
         V("ts", (col(j), col(src), k1, k2, A.mult, A.add), ["KF"], ["K%d" % j])
     V("tt", (col(14), col(4), col(5), A.mult), ["KF"], ["K14"])
-    V("tt", (col(8), col(6), col(7), A.mult), ["K6", "K7"], ["K8"])
     V("tt", (col(11), col(9), col(10), A.mult), ["K9", "K10"], ["K11"])
     V("tt", (col(20), col(19), col(2), A.add), ["K19", "KF"], ["K20"])
     V("tt", (col(23), col(21), col(22), A.add), ["K21", "K22"], ["K23"])
-    V("ts", (col(15), col(14), -15360.0 - 192.0, None, A.mult), ["K14"], ["K15"])
+    V("ts", (col(15), col(14), -15360.0 - 192.0 - 15.0, None, A.mult), ["K14"], ["K15"])
     V("tt", (col(17), col(13), col(16), A.add), ["K13", "K16"], ["K17"])
     V("ts", (col(12), col(11), 0.5, -0.5, A.mult, A.add), ["K11"], ["K12"])
+    V("ts", (col(24), col(14), 0.5, -15.5, A.mult, A.add), ["K14"], ["K24"])
+    V("ts", (col(25), col(14), -32768.0, None, A.mult), ["K14"], ["K25"])
     V("tt", (col(18), col(17), col(15), A.add), ["K17", "K15"], ["K18"])
     V("ts", (T.OFX[:], T.G4[:], col(20), None, A.add), ["G4", "K20"], ["OFX"])
 
@@ -175,26 +184,50 @@ def rank_program(g, core, T, topo):
     V("copy", (T.LX[:, 64 * rank:64 * rank + 64], T.SENDX[:, 64 * rank:64 * rank + 64]), ["SENDX%d" % (rank // 2)], ["LXs"])
     V("copy", (T.LC[:, 16 * rank:16 * rank + 16], T.SENDC[:, 16 * rank:16 * rank + 16]), ["SENDC%d" % (rank // 4)], ["LCs"])
 
+    dma("s", T.PT[:], T.PL[:], "lpt", ["PL", "PLs"], ["PT"])
+    dma("s", T.ST[:], T.SL[:], "lst", ["SL", "SLs"], ["ST"])
+    op("g", "asel", (T.GA[:], T.FOUR[:], [[-16, 8], [0, 4]], A.is_ge, 0.0, 0, 1), ["FOUR"], ["GA"])
+    op("g", "asel", (T.GB[:], T.GA[:], [[16, 8], [0, 4]], A.is_ge, 0.0, 15, -1), ["GA"], ["GB"])
+    V("copy", (T.LW[:, 0:4], T.IC4[:]), ["IC4"], ["LW"])
+    V("copy", (T.OFP[:], T.PT[:]), ["PT"], ["OFP"])
+    op("a", "act", (T.LTR[:, 0:1024], T.LW[:, 0:4].indirect(T.OFP[:, 0:64]), AF.Copy), ["LW", "OFP"], ["LTR0"])
+    V("copy", (T.LTR[:, 1024:2048], T.LW[:, 0:4].indirect(T.OFP[:, 64:128])), ["LW", "OFP"], ["LTR1"])
+    V("copy", (T.PTB[:], T.PT[:]), ["PT"], ["PTB"])
+    V("ts", (T.SELL[:, 0:8], T.GB[:, 0:32:4], 1.0 / 64, None, A.mult), ["GB"], ["SELL"])
+    tau = lambda t: t // 2 + (4 if t % 2 else 0)
+    cs, L0 = [], 1536
+    for t in range(8):
+        o = L0 + 16 * (t // 2) + (128 if t % 2 else 0)
+        for blk in range(2):
+            cs.append((T.PSB[:, o + 8 * blk:o + 8 * blk + 8], T.LTR[:, 256 * t + 128 * blk:256 * t + 128 * blk + 128], T.SELL[:, 0:8], True, True))
+    for t in range(1, 8):
+        o = L0 + 64 + 16 * ((t - 1) // 2) + (0 if t % 2 else 128)
+        cs.append((T.PSB[:, o:o + 16], T.ID[:], T.PTB[:, 16 * t:16 * t + 16], True, True))
+    mms(cs, ["LTR0", "LTR1", "SELL", "PTB", "ID"], ["B3"])
+    V("memset", (T.PSB[:, L0 + 240:L0 + 256], 0.0), ["B3"], ["B3"])
+    for c in range(4):
+        V("ts", (T.AM[:, 128 * c:128 * c + 128], T.PSB[:, L0:L0 + 128], float(c), -float(BIG), A.not_equal, A.mult), ["B3"], ["AM%d" % c])
+    for c in range(4):
+        V("tt", (T.QTB[:, c:512:4], T.PSB[:, L0 + 128:L0 + 256], T.AM[:, 128 * c:128 * c + 128], A.add), ["B3", "AM%d" % c], ["B3", "QTB%d" % c])
+
     for i, k in enumerate((-1.0, -28.0, -896.0, 4096.0)):
         V("ts", (T.HK[:, 128 * i:128 * i + 128], T.ID[:], k, None, A.mult), ["ID"], ["HK"])
     V("memset", (T.ONE2[:], 1.0), [], ["ONE2"])
-    V("memset", (T.FOUR[:], 4.0), [], ["FOUR"])
     V("memset", (T.MK[:], 1.0), [], ["MK0"])
     V("memset", (T.ONE32[:], 1.0), [], ["ONE32"])
     V("memset", (T.BASE[:, 0:1], 0.0), [], ["BASE0"])
     V("memset", (T.TB[:, 3:2048:4], 0.0), [], ["TB3"])
+    V("memset", (T.RST[:], 1.0), [], ["RST0"])
     V("memset", (T.MK[:, 0:512:16], 0.0), ["MK0"], ["MK"])
+    V("memset", (T.RST[:, 0:64:4], 0.0), ["RST0"], ["RST"])
     V("ts", (T.IDN[:], T.ID[:], -1.0, None, A.mult), ["ID"], ["IDN"])
     V("ts", (T.OFF[:], T.G5[:], col(23), None, A.add), ["G5", "K23"], ["OFF"])
-    V("ts", (T.C4[:, 0:4], T.IC4[:], col(3), col(8), A.is_equal, A.mult), ["IC4", "KF", "K8"], ["C4"])
-    V("memset", (T.LR[:], 0.0), [], ["LR"])
+    V("ts", (T.EM[:, 0:4], T.IC4[:], col(3), None, A.is_equal), ["IC4", "KF"], ["EM"])
+    for c in range(4):
+        V("ts", (T.SELY[:, c:32:4], T.GB[:, c:32:4], col(8), T.EM[:, c:c + 1], A.mult, A.mult), ["GB", "K8", "EM"], ["SELY%d" % c])
+        V("ts", (T.SELZ[:, c:32:4], T.GB[:, c:32:4], col(25), T.EM[:, c:c + 1], A.mult, A.mult), ["GB", "K25", "EM"], ["SELZ%d" % c])
     op("g", "asel", (T.TRI[:], T.ONE1[:], [[1, 128]], A.is_ge, 0.0, -1, -1), ["ONE1"], ["TRI"])
     op("g", "asel", (T.SEL[:], T.ONE2[:], [[-16, 8], [0, 8], [-1, 16]], A.is_equal, 0.0, 0, 1), ["ONE2"], ["SEL"])
-    op("g", "asel", (T.GA[:], T.FOUR[:], [[-16, 8]], A.is_ge, 0.0, 0, 1), ["FOUR"], ["GA"])
-    op("g", "asel", (T.GB[:], T.GA[:], [[16, 8]], A.is_ge, 0.0, 15, -1), ["GA"], ["GB"])
-    dma("s", T.PT[:], T.PL[:], "lpt", ["PL", "PLs"], ["PT"])
-    dma("s", T.ST[:], T.SL[:], "lst", ["SL", "SLs"], ["ST"])
-    V("copy", (T.OFP[:], T.PT[:]), ["PT"], ["OFP"])
 
     TAK, TBK = ["TA0", "TA1", "TA2", "TA3"], ["TB0", "TB1", "TB2", "TB3"]
     op("a", "act", (T.LXP[:], T.LX[:, 0:512].indirect(T.OFX[:, 0:32]), AF.Copy), ["LX", "LXs", "OFX"], ["LXP"])
@@ -206,7 +239,6 @@ def rank_program(g, core, T, topo):
         sc = 32.0 / 4 ** i
         op("a", "act", (T.TB[:, i:2048:4], T.LXP[:], AF.Copy), ["LXP"], ["TB%d" % i], scale=sc, bias=sc * B_T[i + 1])
     op("a", "act", (T.HNS[:], T.PSB[:, 0:512], AF.Identity), ["B0"], ["B0", "HNS"], bias=float(BIAS - 16240640))
-    op("a", "act", (T.CM[:], T.C4[:, 0:4].indirect(T.OFP[:, 0:128]), AF.Copy), ["C4", "OFP"], ["CM"])
 
     V("copy", (T.CI[:], T.LC[:]), ["LC", "LCs"], ["CI"])
     for c in range(4):
@@ -240,7 +272,7 @@ def rank_program(g, core, T, topo):
         for i in range(3):
             V("ts", (T.DI[:, 512 * i + n0:512 * i + n1], T.NI[:, n0:n1], 5 * i, 31, A.arith_shift_right, A.bitwise_and), ["NI"], ["DI%d%d" % (i, e)])
         for i in range(3):
-            V("copy", (T.DB[:, m0 + i:m1:4], T.DI[:, 512 * i + n0:512 * i + n1]), ["DI%d%d" % (i, e)], ["DB%d%d" % (i, e)])
+            V("ts", (T.DB[:, m0 + i:m1:4], T.DI[:, 512 * i + n0:512 * i + n1], -15.5, None, A.add), ["DI%d%d" % (i, e)], ["DB%d%d" % (i, e)])
         for bk in (2 * e, 2 * e + 1):
             mms([(T.PSA[:, 128 * il:128 * il + 128], T.DB[:, 128 * il:128 * il + 128], T.ID[:], e == 1, e == 1 or il % 4 == 3) for il in range(4 * bk, 4 * bk + 4)],
                 ["DB%d%d" % (i, e) for i in (3, 0, 1, 2)] + ["ID"], ["A%d" % bk])
@@ -250,7 +282,7 @@ def rank_program(g, core, T, topo):
                     V("tt", (o, x, T.XL[:, 128 * il:128 * il + 128], A.add), ["A%d" % bk, "XL%d" % bk], ["A%d" % bk, XCK[bk]])
                 else:
                     op("a", "act", (o, x, AF.Copy), ["A%d" % bk], ["A%d" % bk, XCK[bk]])
-    XK, LK = ["XE"], ["LR%d" % y for y in range(8)]
+    XK = ["XE"]
     for k in range(NPE, 8):
         for y in range(8):
             dma("s", T.X[16 * y:16 * y + 16, 2048 * k:2048 * k + 2048], T.XC[16 * k:16 * k + 16, :], "rep", XCK, ["XD%d%d" % (k, y)])
@@ -269,65 +301,80 @@ def rank_program(g, core, T, topo):
             n += 1
             if n == 2:
                 V("ts", (T.G3[:], T.G1[:], col(1), None, A.is_gt), ["G1", "KF"], ["G3"])
-                V("ts", (T.QT[:], T.PT[:], 1.0, None, A.mult), ["PT"], ["QT"])
                 V("ts", (T.ST4[:], T.ST[:], 4.0, None, A.mult), ["ST"], ["ST4"])
-                V("ts", (T.EM[:, 0:4], T.IC4[:], col(3), None, A.is_equal), ["IC4", "KF"], ["EM"])
                 V("tt", (T.EV[:, 0:4], T.EM[:, 0:4], T.BASE[:, 8:33:8], A.mult), ["EM", "BASE"], ["EV"])
             if n == 4:
-                V("tt", (T.W[:], T.G3[:], T.G2[:], A.mult), ["G3", "G2"], ["W"])
+                V("tt", (T.WF[:], T.G3[:], T.G2[:], A.mult), ["G3", "G2"], ["WF"])
                 for h in range(2):
                     V("tt", (T["I%d" % h][:], T.ST4[:, 16 * h:16 * h + 16], T.PT[:, 0:16], A.add), ["ST4", "PT"], ["I%d" % h])
                 V("red", (T.EV[:, 4:5], T.EV[:, 0:4], AxisListType.X, A.add), ["EV"], ["EV4"])
-            if n in (6, 8):
-                for y in range(2 * n - 12, 2 * n - 8):
-                    V("ts", (T.LR[:, 16 * y:16 * y + 1936:129], T.ONE1[:, 0:16], T.GB[:, y:y + 1], None, A.mult), ["ONE1", "GB", "LR"], [LK[y]])
             if n == 6:
+                V("ts", (T.W[:], T.WF[:], -1.0, None, A.add), ["WF"], ["W"])
                 V("ts", (T.EV[:, 5:6], T.EV[:, 4:5], float(BIAS), col(11), A.add, A.mult), ["EV4", "K11"], ["EV5"])
             if n == 8:
                 V("ts", (T.EI[:, 0:1], T.EV[:, 5:6], col(12), None, A.add), ["EV5", "K12"], ["EI0"])
             if n == 10:
                 V("ts", (T.EI[:, 1:2], T.EI[:, 0:1], 31, None, A.bitwise_and), ["EI0"], ["EI1"])
             if n == 12:
-                V("copy", (T.X[:, 16384:16385], T.EI[:, 1:2]), ["EI1"], ["XE"])
+                V("ts", (T.X[:, 16384:16385], T.EI[:, 1:2], col(24), None, A.add), ["EI1", "K24"], ["XE"])
 
-    def small(n):
-        t, h = n // 2, n % 2
-        s = str(h)
-        I, J, O = T["I" + s], T["J" + s], T["O" + s]
-        ps, pk = 512 * h, "A" + s
-        if n >= 2:
-            op("a", "act", (T["U" + s][:], T.PSA[:, ps:ps + 16], AF.Identity), [pk], [pk, "U" + s], bias=-4.0 * BIAS)
-            V("tt", (I[:], T.PSA[:, ps + 16:ps + 32], T["U" + s][:], A.add), [pk, "U" + s], [pk, "I" + s])
-        if t < 8:
-            V("ts", (J[:, 0:16], I[:], 6, 0x7FFF, A.arith_shift_right, A.bitwise_and), ["I" + s], ["J" + s])
-            V("ts", (J[:, 16:32], I[:], 63, None, A.bitwise_and), ["I" + s], ["J" + s])
-            V("copy", (O[:], J[:]), ["J" + s], ["O" + s])
-            op("a", "act", (T["Z" + s][:], T.X[:, 0:16385].indirect(O[:, 0:16]), AF.Identity), ["O" + s] + XK, ["Z" + s], bias=6128.5)
+    B = lambda name, n: T[("S1B" if name == "S" and n % 2 else "%s%d" % (name, n % 2))]
+    key = lambda name, n: "%s:%d" % (name, n % 2)
+    for h in range(2):
+        last["I:%d" % h] = last["I%d" % h]
+
+    def state(n):
+        ps, pk = 512 * (n % 2), "A%d" % (n % 2)
+        V("scan", (B("S", n)[:], T.RST[:], T.PSA[:, ps:ps + 64], 0.0, A.mult, A.max), [pk, "RST"], [pk, key("S", n)])
+
+    def block(n):
+        o = B("OA", n)[:]
+        if n < 2:
+            V("ts", (o, B("I", n)[:], 1.0 / 64, -0.5 + 0.5 / 64, A.mult, A.add), [key("I", n)], [key("OA", n)])
         else:
-            V("ts", (J[:, 0:16], I[:], 2, 0x7FFFF, A.arith_shift_right, A.bitwise_and), ["I" + s], ["J" + s])
-            V("copy", (T.RES[:, 16 * h:16 * h + 16], J[:, 0:16]), ["J" + s], ["RES%d" % h])
+            V("ts", (o, B("S", n)[:, 3:64:4], 1.0 / 64, -0.5 - 1.5 / 64, A.mult, A.add), [key("S", n)], [key("OA", n)])
+        op("a", "act", (B("Z", n)[:], T.X[:, 0:16385].indirect(B("OA", n)[:, 0:16]), AF.Copy), [key("OA", n)] + XK, [key("Z", n)])
 
-    def big(n):
-        t, h = n // 2, n % 2
-        s = str(h)
-        O, YE, ps = T["O" + s], T["YE" + s], 512 * h
-        V("tt", (YE[:, 0:256], T.X[:, 0:16385].indirect(O[:, 0:16]), T.CM[:, 256 * t:256 * t + 256], A.mult), ["O" + s, "CM"] + XK, ["Y" + s])
-        V("tt", (YE[:, 256:512], T.W[:, 0:64].indirect(O[:, 16:32]), T["Z" + s][:], A.is_equal), ["O" + s, "W", "Z" + s], ["E" + s])
-        cs = [(T.PSA[:, ps:ps + 32], T.LR[:, 128 * r:128 * r + 128], YE[:, r:512:16], r == 0, r == 15) for r in range(16)]
-        if t < 7:
-            cs.insert(1, (T.PSA[:, ps:ps + 16], T.ID[:], T.QT[:, 16 * t + 16:16 * t + 32], False, False))
-        mms(cs, ["Y" + s, "E" + s, "QT", "ID"] + LK, ["A" + s])
+    def table(n):
+        t, ps, pk, Z = n // 2, 512 * (n % 2), "A%d" % (n % 2), B("Z", n)
+        q0 = 64 * tau(t)
+        cs = [(T.PSA[:, ps:ps + 64], T.ID[:], T.QTB[:, q0:q0 + 64], True, False)]
+        cs += [(T.PSA[:, ps + 32 * k:ps + 32 * k + 32], Z[:, 128 * k:128 * k + 128], T.SELY[:], False, False) for k in range(2)]
+        mms(cs, [key("Z", n), "ID"] + ["QTB%d" % c for c in range(4)] + ["SELY%d" % c for c in range(4)], [pk])
+        V("ts", (B("ZL", n)[:], Z[:], RND, RND, A.add, A.subtract), [key("Z", n)], [key("ZL", n)])
+
+    def count(n):
+        ps, pk, ZL, E = 512 * (n % 2), "A%d" % (n % 2), B("ZL", n), B("E", n)
+        mms([(T.PSA[:, ps + 32 * k:ps + 32 * k + 32], ZL[:, 128 * k:128 * k + 128], T.SELZ[:], False, False) for k in range(2)],
+            [key("ZL", n)] + ["SELZ%d" % c for c in range(4)], [pk])
+        V("tt", (E[:], T.W[:, 0:64].indirect(B("OB", n)[:, 0:16]), ZL[:], A.is_equal), [key("OB", n), "W", key("ZL", n)], [key("E", n)])
+        mms([(T.PSA[:, ps + 32 * k:ps + 32 * k + 32], E[:, 128 * k:128 * k + 128], T.GB[:], False, k == 1) for k in range(2)],
+            [key("E", n), "GB"], [pk])
 
     for n in range(18):
+        if n >= 2:
+            state(n)
         if 0 < n < 17:
-            big(n - 1)
-        small(n)
-    send(lambda d: T.RES[:], T.FL[rank], "arrF", "locF", ["RES0", "RES1"])
+            table(n - 1)
+        if n < 16:
+            block(n)
+            if n >= 2:
+                V("ts", (B("I", n)[:], B("S", n)[:, 3:64:4], -2.0, None, A.add), [key("S", n)], [key("I", n)])
+        else:
+            h = n % 2
+            V("ts", (T.RES[:, 16 * h:16 * h + 16], B("S", n)[:, 3:64:4], 0.25, -0.5, A.mult, A.add), [key("S", n)], ["RES%d" % h])
+        if 0 < n < 17:
+            count(n - 1)
+        if n < 16:
+            V("ts", (B("J", n)[:], B("I", n)[:], 63, None, A.bitwise_and), [key("I", n)], [key("J", n)])
+            V("copy", (B("OB", n)[:], B("J", n)[:]), [key("J", n)], [key("OB", n)])
+    dma("s", T.RD[:], T.RES[:], "rd", ["RES0", "RES1"], ["RD"])
+    send(lambda d: T.RD[d], T.FL[rank], "arrF", "locF", ["RD"])
     r0, r1 = 16 * rank, 16 * rank + 16
     dma("s", T.y[r0:r1, :], T.RES[r0:r1, :], "yself", ["RES0", "RES1"], ["y0"])
     if rank > 0:
-        dma("s", T.y[0:r0, :], T.FL[0:rank, r0:r1, :], "yout", ["FL"], ["y1"])
+        dma("s", T.y[0:r0, :], T.FL[0:rank], "yout", ["FL"], ["y1"])
     if rank < 7:
-        dma("s", T.y[r1:128, :], T.FL[rank + 1:8, r0:r1, :], "yout", ["FL"], ["y2"])
+        dma("s", T.y[r1:128, :], T.FL[rank + 1:8], "yout", ["FL"], ["y2"])
     for sem in sorted(total):
         wait("g", (sem, total[sem], {}))

@@ -3,10 +3,14 @@ from concourse.bass import DstId, RemoteDMATransfer
 from concourse.mybir import AluOpType as A, AxisListType, ActivationFunctionType as AF
 
 NPE = 4
-BIAS = 507904
 BIG = 2097152
-RND = 402653184.0
+RND = 12582912.0
 B_T = (0.0, 638.5, 2552.5, 10208.5)
+P0 = "aA0 aA1 aB0 aA2 aB1 vA3 vB2"
+P1 = "aA0 aA1 aB0"
+P2 = "aA2 aB1 aA3 aB2"
+XCQ = "aava"
+XQ = "ava" + "avavavavavavavav" * 2
 
 SCRATCH = {
     "PP": ("dram", [8, 128, 16], "int32"), "SS": ("dram", [8, 128, 4], "int32"),
@@ -15,20 +19,20 @@ SCRATCH = {
     "PSA": ("psum", [128, 2048], "float32"), "PSB": ("psum", [128, 2048], "float32"),
 }
 for _n, _w, _d in (
-        ("D32", 2048, "int32"), ("D", 2048, "bfloat16"), ("CE", 2048, "bfloat16"), ("SENDX", 512, "bfloat16"),
-        ("SENDC", 128, "float32"), ("LX", 512, "bfloat16"), ("LC", 128, "float32"), ("LXP", 512, "bfloat16"),
+        ("D32", 2048, "int32"), ("D", 2048, "bfloat16"), ("CE", 2048, "bfloat16"), ("SEND", 384, "float32"), ("LR", 384, "float32"),
+        ("H", 256, "float32"), ("HM", 256, "float32"), ("LXP", 512, "bfloat16"),
         ("TA", 2048, "bfloat16"), ("TB", 2048, "bfloat16"), ("CI", 128, "int32"), ("CX", 512, "int32"), ("NS", 512, "float32"),
         ("S1", 512, "bfloat16"), ("N15", 32, "bfloat16"), ("MK", 512, "float32"), ("BASE", 40, "float32"),
-        ("ONE32", 32, "float32"), ("F", 512, "float32"), ("HNS", 512, "float32"), ("NI", 512, "int32"), ("DI", 2048, "int32"),
-        ("DB", 2048, "bfloat16"), ("XL", 2048, "bfloat16"), ("XC", 2048, "bfloat16"), ("X", 16400, "bfloat16"),
-        ("ONE1", 128, "bfloat16"), ("ONE2", 1024, "bfloat16"), ("FOUR", 32, "bfloat16"), ("GA", 32, "bfloat16"), ("GB", 32, "bfloat16"),
-        ("ID", 128, "bfloat16"), ("IDN", 128, "bfloat16"), ("PK", 512, "bfloat16"),
-        ("HK", 512, "bfloat16"), ("TRI", 128, "bfloat16"), ("SEL", 1024, "bfloat16"),
+        ("ONE32", 32, "float32"), ("F", 512, "float32"), ("NI", 512, "int32"), ("DI", 1024, "int32"),
+        ("DB", 2048, "bfloat16"), ("XC", 2048, "bfloat16"), ("X", 16400, "bfloat16"),
+        ("ONE1", 128, "bfloat16"), ("ONE2", 512, "bfloat16"), ("FOUR", 32, "bfloat16"), ("GA", 32, "bfloat16"), ("GB", 32, "bfloat16"),
+        ("ID", 128, "bfloat16"), ("IDP", 128, "bfloat16"), ("IDN", 128, "bfloat16"), ("INI", 128, "bfloat16"), ("CON", 64, "bfloat16"),
+        ("PK", 1024, "bfloat16"), ("TRI", 128, "bfloat16"), ("SEL", 128 * NPE, "bfloat16"),
         ("SELY", 32, "bfloat16"), ("SELZ", 32, "bfloat16"), ("SELL", 16, "bfloat16"),
-        ("KI", 8, "int32"), ("KF", 32, "float32"), ("G1", 64, "float32"),
-        ("G2", 64, "float32"), ("G3", 64, "float32"), ("G4", 32, "float32"), ("G5", 32, "float32"), ("IC4", 4, "float32"),
-        ("EM", 8, "float32"), ("EV", 8, "float32"), ("EI", 4, "int32"), ("WF", 64, "float32"), ("W", 64, "bfloat16"), ("LW", 16, "bfloat16"),
-        ("OFX", 32, "uint16"), ("OFF", 32, "uint16"), ("PT", 128, "int32"), ("ST", 32, "int32"), ("ST4", 32, "int32"),
+        ("KI", 16, "int32"), ("KF", 48, "float32"), ("G1", 64, "float32"),
+        ("G2", 64, "float32"), ("G3", 64, "float32"), ("G4", 16, "float32"), ("G5", 32, "float32"), ("G6", 8, "float32"), ("IC4", 4, "float32"),
+        ("EM", 8, "float32"), ("EV", 8, "float32"), ("EI", 4, "int32"), ("W", 64, "bfloat16"), ("LW", 16, "bfloat16"),
+        ("OFX", 16, "uint16"), ("OFF", 32, "uint16"), ("OFC", 8, "uint16"), ("PT", 128, "int32"), ("ST", 32, "int32"), ("ST4", 32, "int32"),
         ("OFP", 128, "uint16"), ("PTB", 128, "bfloat16"), ("LTR", 2048, "bfloat16"), ("AM", 512, "bfloat16"), ("QTB", 512, "bfloat16"),
         ("RST", 64, "float32"), ("RES", 32, "float32"),
         ("I0", 16, "int32"), ("J0", 16, "int32"), ("OA0", 16, "uint16"), ("OB0", 16, "uint16"), ("S0", 64, "float32"),
@@ -37,7 +41,22 @@ for _n, _w, _d in (
         ("Z1", 256, "bfloat16"), ("ZL1", 256, "bfloat16"), ("E1", 256, "bfloat16")):
     SCRATCH[_n] = ("sbuf", [128, _w], _d)
 SEMAPHORES = (["vq", "aq", "pq", "gq", "dp", "ds", "dsp", "dss", "lpt", "lst", "rep", "yself", "yout", "rd",
-               "arrP", "arrS", "arrX", "arrC", "arrF", "locP", "locS", "locX", "locC", "locF"] + ["b%d" % _i for _i in range(8)])
+               "arrP", "arrS", "arrX", "arrF", "locP", "locS", "locX", "locF"] + ["b%d" % _i for _i in range(8)])
+
+
+def plan(T, topo, rank, kind):
+    core = T.cores[rank]
+    off = [d for d in range(8) if d != rank and topo.chip(T.cores[d]) != topo.chip(core)]
+    on = [d for d in range(8) if d != rank and topo.chip(T.cores[d]) == topo.chip(core)]
+    off.sort(key=lambda d: (topo.same_plane(topo.chip(core), topo.chip(T.cores[d])), (d - rank) % 8))
+    eo = topo.engines(core, T.cores[off[0]])
+    en = [e for e in topo.engines(core, T.cores[on[0]]) if e not in eo]
+    if kind == "X":
+        c1 = [(d, eo[2 * i:2 * i + 2]) for i, d in enumerate(off[:4])]
+        c2 = [(d, eo[4 * i:4 * i + 4]) for i, d in enumerate(off[4:])] + [(d, en[:2]) for d in on]
+        return [c1, c2]
+    sh = 2 if kind == "S" else 0
+    return [[(d, [eo[i + sh]]) for i, d in enumerate(off)] + [(d, [en[sh // 2]]) for d in on]]
 
 
 def rank_program(g, core, T, topo):
@@ -104,29 +123,36 @@ def rank_program(g, core, T, topo):
         total[sem] = total.get(sem, 0) + 16
         mark((sem, None, dict(known[q])), rd, wr)
 
-    def send(src, dst, arr, loc, rd):
+    def send(kind, src, dst, arr, loc, rd):
         deps("g", rd, [])
-        tr, used = [], set()
-        peers = sorted([d for d in range(8) if d != rank], key=lambda d: len(topo.engines(core, T.cores[d])))
-        for d in peers:
-            dc = T.cores[d]
-            e = [e for e in topo.engines(core, dc) if e not in used][0]
-            used.add(e)
-            rid, pid, _ = topo.addr(dc)
-            tr.append(RemoteDMATransfer(dst_ids=[DstId(rid=rid, pnc=pid)], dma_engine_mask=1 << e, remote_sem=T.sem[arr], srcs=[src(d)], dsts=[dst]))
-        g.remote_dma_fused(tr, local_sem=T.sem[loc])
-        total[loc] = 7
-        total[arr] = 7
-        mark((loc, 7, dict(known["g"])), rd, [])
+        for call in plan(T, topo, rank, kind):
+            tr = []
+            for d, es in call:
+                rid, pid, _ = topo.addr(T.cores[d])
+                tr.append(RemoteDMATransfer(dst_ids=[DstId(rid=rid, pnc=pid)], dma_engine_mask=sum(1 << e for e in es),
+                                            remote_sem=T.sem[arr], srcs=[src(d)], dsts=[dst]))
+                total[loc] = total.get(loc, 0) + len(es)
+            g.remote_dma_fused(tr, local_sem=T.sem[loc])
+        total[arr] = arrive[arr]
+        mark((loc, total[loc], dict(known["g"])), rd, [])
 
+    arrive = {}
+    for kind, k, arr in (("P", "PL", "arrP"), ("S", "SL", "arrS"), ("X", "LR", "arrX"), ("F", "FL", "arrF")):
+        arrive[arr] = sum(len(es) for r in range(8) if r != rank for call in plan(T, topo, r, kind) for d, es in call if d == rank)
+        last[k] = (arr, arrive[arr], {})
     V = lambda name, args, rd, wr: op("v", name, args, rd, wr)
-    for k, arr in (("PL", "arrP"), ("SL", "arrS"), ("LX", "arrX"), ("LC", "arrC"), ("FL", "arrF")):
-        last[k] = (arr, 7, {})
+    S = lambda name, args, rd, wr, **kw: op("a", name, args, rd, wr, **kw)
+
+    def cp(q, out, in_, rd, wr):
+        if q == "v":
+            V("copy", (out, in_), rd, wr)
+        else:
+            S("act", (out, in_, AF.Copy), rd, wr)
 
     dma("s", T.PP[:], T.pats[:], "dp", [], ["PP"])
     dma("s", T.SS[:], T.starts[:], "ds", [], ["SS"])
     for s in range(8):
-        dma("s" if s % 2 == 0 else "a", T.D32[:, 256 * s:256 * s + 256], T.bwt[s:s + 1, :], "b%d" % s, [], ["D32%d" % s])
+        dma("s" if s in (3, 5, 6, 7) else "a", T.D32[:, 256 * s:256 * s + 256], T.bwt[s:s + 1, :], "b%d" % s, [], ["D32%d" % s])
     dma("s", T.PL[rank], T.pats[16 * rank:16 * rank + 16, :], "dsp", [], ["PLs"])
     dma("s", T.SL[rank], T.starts[16 * rank:16 * rank + 16, :], "dss", [], ["SLs"])
 
@@ -135,67 +161,97 @@ def rank_program(g, core, T, topo):
     V("memset", (T.FOUR[:], 4.0), [], ["FOUR"])
     op("g", "iota", (T.KI[:, 0:1], [[0, 1]], 0, 1), [], ["KI0"])
     op("g", "asel", (T.ID[:], T.ONE1[:], [[-1, 128]], A.is_equal, 0.0, 0, 1), ["ONE1"], ["ID"])
-    op("g", "iota", (T.G4[:], [[4, 16], [256, 2]], 0, 0), [], ["G4"], **fl)
-    op("g", "iota", (T.G5[:], [[1, 16], [64, 2]], 0, 0), [], ["G5"], **fl)
-    op("g", "iota", (T.G1[:], [[1, 16], [0, 4]], 0, 0), [], ["G1"], **fl)
-    op("g", "iota", (T.G2[:], [[0, 16], [32, 4]], 1, 0), [], ["G2"], **fl)
+    op("g", "iota", (T.G4[:], [[2, 4], [8, 4]], 0, 0), [], ["G4"], **fl)
+    op("g", "iota", (T.G5[:], [[1, 4], [4, 4], [64, 2]], 0, 0), [], ["G5"], **fl)
+    op("g", "iota", (T.G6[:], [[48, 8]], 32, 0), [], ["G6"], **fl)
     op("g", "iota", (T.IC4[:], [[1, 4]], 0, 0), [], ["IC4"], **fl)
-    send(lambda d: T.PP[d], T.PL[rank], "arrP", "locP", ["PP"])
-    send(lambda d: T.SS[d], T.SL[rank], "arrS", "locS", ["SS"])
-    for d, n, sh in ((1, 15, 0), (2, 3, 0), (3, 3, 2), (4, 1, 0), (5, 1, 1)):
-        V("ts", (T.KI[:, d:d + 1], T.KI[:, 0:1], sh, n, A.arith_shift_right, A.bitwise_and), ["KI0"], ["KI"])
-    V("copy", (T.KF[:, 0:6], T.KI[:, 0:6]), ["KI", "KI0"], ["KF"])
+    send("P", lambda d: T.PP[d], T.PL[rank], "arrP", "locP", ["PP"])
+    send("S", lambda d: T.SS[d], T.SL[rank], "arrS", "locS", ["SS"])
+    op("g", "asel", (T.GA[:], T.FOUR[:], [[-16, 8], [0, 4]], A.is_ge, 0.0, 0, 1), ["FOUR"], ["GA"])
+    op("g", "asel", (T.GB[:], T.GA[:], [[16, 8], [0, 4]], A.is_ge, 0.0, 15, -1), ["GA"], ["GB"])
+    op("g", "asel", (T.TRI[:], T.ONE1[:], [[1, 128]], A.is_ge, 0.0, -1, -1), ["ONE1"], ["TRI"])
+    op("g", "iota", (T.G1[:], [[1, 16], [0, 4]], 0, 0), [], ["G1"], **fl)
+    op("g", "iota", (T.G2[:], [[0, 16], [64, 4]], 12288, 0), [], ["G2"], **fl)
+
     col = lambda j: T.KF[:, j:j + 1]
-    op("a", "act", (col(8), col(2), AF.Exp), ["KF"], ["K8"], scale=float(np.log(32.0)))
-    for i in range(4):
+    for d, n, sh in ((2, 3, 0), (1, 15, 0), (3, 3, 2), (4, 1, 0), (5, 1, 1), (6, 7, 1), (7, 1, 0)):
+        V("ts", (T.KI[:, d:d + 1], T.KI[:, 0:1], sh, n, A.arith_shift_right, A.bitwise_and), ["KI0"], ["KI"])
+    V("copy", (T.KF[:, 0:8], T.KI[:, 0:8]), ["KI", "KI0"], ["KF"])
+    S("act", (col(8), col(2), AF.Exp), ["KF"], ["K8"], scale=float(np.log(64.0)))
+    for i in range(8):
         V("ts", (T.PK[:, 128 * i:128 * i + 128], T.ID[:], float(4 ** i), None, A.mult), ["ID"], ["PK"])
-    for j, src, k1, k2 in ((19, 3, 64.0, 0.0), (13, 4, -5120.0, 20480.0), (16, 5, -5120.0, 0.0),
-                           (9, 4, -31.0 / 32, 1.0), (10, 5, -1023.0 / 1024, 1.0), (21, 2, 128.0, 0.0), (22, 3, 16.0, 0.0)):
-        V("ts", (col(j), col(src), k1, k2, A.mult, A.add), ["KF"], ["K%d" % j])
-    V("tt", (col(14), col(4), col(5), A.mult), ["KF"], ["K14"])
-    V("tt", (col(11), col(9), col(10), A.mult), ["K9", "K10"], ["K11"])
-    V("tt", (col(20), col(19), col(2), A.add), ["K19", "KF"], ["K20"])
-    V("tt", (col(23), col(21), col(22), A.add), ["K21", "K22"], ["K23"])
-    V("ts", (col(15), col(14), -15360.0 - 192.0 - 15.0, None, A.mult), ["K14"], ["K15"])
-    V("tt", (col(17), col(13), col(16), A.add), ["K13", "K16"], ["K17"])
-    V("ts", (col(12), col(11), 0.5, -0.5, A.mult, A.add), ["K11"], ["K12"])
-    V("ts", (col(24), col(14), 0.5, -15.5, A.mult, A.add), ["K14"], ["K24"])
-    V("ts", (col(25), col(14), -32768.0, None, A.mult), ["K14"], ["K25"])
-    V("tt", (col(18), col(17), col(15), A.add), ["K17", "K15"], ["K18"])
-    V("ts", (T.OFX[:], T.G4[:], col(20), None, A.add), ["G4", "K20"], ["OFX"])
+
+    def lin(j, src, k1, k2):
+        V("ts", (col(j), col(src), k1, k2, A.mult, A.add), ["KF"] if src < 8 else ["K%d" % src], ["K%d" % j])
 
     CH = 5.0 * float(np.log(2.0))
     for s in range(8):
         c0 = 256 * s
         V("copy", (T.D[:, c0:c0 + 256], T.D32[:, c0:c0 + 256]), ["D32%d" % s], ["D%d" % s])
-        op("a", "act", (T.CE[:, c0:c0 + 256], T.D[:, c0:c0 + 256], AF.Exp), ["D%d" % s], ["CE%d" % s], scale=CH)
+        S("act", (T.CE[:, c0:c0 + 256], T.D[:, c0:c0 + 256], AF.Exp), ["D%d" % s], ["CE%d" % s], scale=CH)
     for f in range(4):
         lo, hi = 512 * f, 512 * f + 512
-        mms([(T.PSA[:, lo:lo + 128], T.PK[:, 128 * i:128 * i + 128], T.D[:, lo + i:hi:4], i == 0, i == 3) for i in range(4)],
+        mms([(T.PSA[:, lo:lo + 64], T.PK[:, 128 * i:128 * i + 128], T.D[:, lo + i:hi:8], i == 0, i == 7) for i in range(8)],
             ["D%d" % (2 * f), "D%d" % (2 * f + 1), "PK"], ["A%d" % f])
-        V("copy", (T.SENDX[:, 128 * f:128 * f + 128], T.PSA[:, lo:lo + 128]), ["A%d" % f], ["A%d" % f, "SENDX%d" % f])
-    send(lambda d: T.SENDX[:, 64 * d:64 * d + 64], T.LX[:, 64 * rank:64 * rank + 64], "arrX", "locX", ["SENDX%d" % f for f in range(4)])
+        if f % 2 == 1:
+            hh = f // 2
+            lo, hi, o = 1024 * hh, 1024 * hh + 1024, 512 * hh
+            mms([(T.PSB[:, o:o + 64], T.ID[:], T.CE[:, lo + q:hi:16], q == 0, q == 15) for q in range(16)],
+                ["CE%d" % s for s in range(4 * hh, 4 * hh + 4)] + ["ID"], ["B%d" % hh])
+    sk = []
+    for f in range(4):
+        for s in (2 * f, 2 * f + 1):
+            o = 512 * f + 32 * (s % 2)
+            V("ts", (T.SEND[:, 48 * s:48 * s + 32], T.PSA[:, o:o + 32], 128.0, None, A.add), ["A%d" % f], ["SX%d" % s])
+            sk.append("SX%d" % s)
     for hh in range(2):
-        lo, hi, o = 1024 * hh, 1024 * hh + 1024, 512 * hh
-        mms([(T.PSB[:, o:o + 64], T.ID[:], T.CE[:, lo + q:hi:16], q == 0, q == 15) for q in range(16)],
-            ["CE%d" % s for s in range(4 * hh, 4 * hh + 4)] + ["ID"], ["B%d" % hh])
-        V("copy", (T.SENDC[:, 64 * hh:64 * hh + 64], T.PSB[:, o:o + 64]), ["B%d" % hh], ["B%d" % hh, "SENDC%d" % hh])
-    send(lambda d: T.SENDC[:, 16 * d:16 * d + 16], T.LC[:, 16 * rank:16 * rank + 16], "arrC", "locC", ["SENDC0", "SENDC1"])
-    V("copy", (T.LX[:, 64 * rank:64 * rank + 64], T.SENDX[:, 64 * rank:64 * rank + 64]), ["SENDX%d" % (rank // 2)], ["LXs"])
-    V("copy", (T.LC[:, 16 * rank:16 * rank + 16], T.SENDC[:, 16 * rank:16 * rank + 16]), ["SENDC%d" % (rank // 4)], ["LCs"])
+        for s in (4 * hh, 4 * hh + 1, 4 * hh + 2, 4 * hh + 3):
+            o = 512 * hh + 16 * (s % 4)
+            cp("a" if hh == 0 else "v", T.SEND[:, 48 * s + 32:48 * s + 48], T.PSB[:, o:o + 16], ["B%d" % hh], ["SC%d" % s])
+            sk.append("SC%d" % s)
+    send("X", lambda d: T.SEND[:, 48 * d:48 * d + 48], T.LR[:, 48 * rank:48 * rank + 48], "arrX", "locX", sk)
+    V("copy", (T.LR[:, 48 * rank:48 * rank + 48], T.SEND[:, 48 * rank:48 * rank + 48]), ["SX%d" % rank, "SC%d" % rank], ["LRs"])
+
+    V("memset", (T.ONE2[:], 1.0), [], ["ONE2"])
+    op("g", "asel", (T.SEL[:], T.ONE2[:, 0:128 * NPE], [[-16, NPE], [0, 8], [-1, 16]], A.is_equal, 0.0, 0, 1), ["ONE2"], ["SEL"])
+    lin(28, 6, 48.0, 0.0)
+    lin(21, 2, 128.0, 0.0)
+    lin(22, 3, 16.0, 0.0)
+    lin(13, 4, -12800.0, 51200.0)
+    lin(16, 5, -13056.0, 0.0)
+    V("tt", (col(14), col(4), col(5), A.mult), ["KF"], ["K14"])
+    V("tt", (col(29), col(28), col(7), A.add), ["K28", "KF"], ["K29"])
+    V("tt", (col(23), col(21), col(22), A.add), ["K21", "K22"], ["K23"])
+    V("tt", (col(17), col(13), col(16), A.add), ["K13", "K16"], ["K17"])
+    lin(15, 14, -38144.0, 0.0)
+    lin(31, 14, -1.0, 1.0)
+    V("ts", (T.OFX[:], T.G4[:], col(29), None, A.add), ["G4", "K29"], ["OFX"])
+    V("ts", (T.OFC[:], T.G6[:], col(1), None, A.add), ["G6", "KF"], ["OFC"])
+    V("ts", (T.OFF[:], T.G5[:], col(23), None, A.add), ["G5", "K23"], ["OFF"])
+    V("tt", (col(18), col(17), col(15), A.add), ["K17", "K15"], ["K18"])
+    V("memset", (T.MK[:], 1.0), [], ["MK0"])
+    V("memset", (T.ONE32[:], 1.0), [], ["ONE32"])
+    V("memset", (T.BASE[:, 0:1], 0.0), [], ["BASE0"])
+    V("ts", (T.INI[:], T.ID[:], col(18), None, A.mult), ["ID", "K18"], ["INI"])
+    V("memset", (T.TB[:, 3:2048:4], 0.0), [], ["TB3"])
+    V("memset", (T.DB[:, 3:2048:4], 0.0), [], ["DB3"])
+    V("ts", (T.IDP[:], T.ID[:], 1.25, None, A.mult), ["ID"], ["IDP"])
+    V("ts", (T.IDN[:], T.ID[:], -1.25, None, A.mult), ["ID"], ["IDN"])
+    V("memset", (T.MK[:, 0:512:16], 0.0), ["MK0"], ["MK"])
+    V("copy", (T.LW[:, 0:4], T.IC4[:]), ["IC4"], ["LW"])
+    V("ts", (T.SELL[:, 0:8], T.GB[:, 0:32:4], 1.0 / 64, None, A.mult), ["GB"], ["SELL"])
+    L0 = 1536
+    V("memset", (T.PSB[:, L0 + 240:L0 + 256], 0.0), [], ["B3z"])
+    mms([(T.PSA[:, 512 * b:512 * b + 512], T.INI[:], T.ONE2[:, 0:512], True, False) for b in range(4)], ["INI", "ONE2"], ["A0", "A1", "A2", "A3"])
 
     dma("s", T.PT[:], T.PL[:], "lpt", ["PL", "PLs"], ["PT"])
     dma("s", T.ST[:], T.SL[:], "lst", ["SL", "SLs"], ["ST"])
-    op("g", "asel", (T.GA[:], T.FOUR[:], [[-16, 8], [0, 4]], A.is_ge, 0.0, 0, 1), ["FOUR"], ["GA"])
-    op("g", "asel", (T.GB[:], T.GA[:], [[16, 8], [0, 4]], A.is_ge, 0.0, 15, -1), ["GA"], ["GB"])
-    V("copy", (T.LW[:, 0:4], T.IC4[:]), ["IC4"], ["LW"])
     V("copy", (T.OFP[:], T.PT[:]), ["PT"], ["OFP"])
-    op("a", "act", (T.LTR[:, 0:1024], T.LW[:, 0:4].indirect(T.OFP[:, 0:64]), AF.Copy), ["LW", "OFP"], ["LTR0"])
-    V("copy", (T.LTR[:, 1024:2048], T.LW[:, 0:4].indirect(T.OFP[:, 64:128])), ["LW", "OFP"], ["LTR1"])
     V("copy", (T.PTB[:], T.PT[:]), ["PT"], ["PTB"])
-    V("ts", (T.SELL[:, 0:8], T.GB[:, 0:32:4], 1.0 / 64, None, A.mult), ["GB"], ["SELL"])
+    S("act", (T.LTR[:, 0:1024], T.LW[:, 0:4].indirect(T.OFP[:, 0:64]), AF.Copy), ["LW", "OFP"], ["LTR0"])
+    V("copy", (T.LTR[:, 1024:2048], T.LW[:, 0:4].indirect(T.OFP[:, 64:128])), ["LW", "OFP"], ["LTR1"])
     tau = lambda t: t // 2 + (4 if t % 2 else 0)
-    cs, L0 = [], 1536
+    cs = []
     for t in range(8):
         o = L0 + 16 * (t // 2) + (128 if t % 2 else 0)
         for blk in range(2):
@@ -203,150 +259,154 @@ def rank_program(g, core, T, topo):
     for t in range(1, 8):
         o = L0 + 64 + 16 * ((t - 1) // 2) + (0 if t % 2 else 128)
         cs.append((T.PSB[:, o:o + 16], T.ID[:], T.PTB[:, 16 * t:16 * t + 16], True, True))
-    mms(cs, ["LTR0", "LTR1", "SELL", "PTB", "ID"], ["B3"])
-    V("memset", (T.PSB[:, L0 + 240:L0 + 256], 0.0), ["B3"], ["B3"])
-    for c in range(4):
-        V("ts", (T.AM[:, 128 * c:128 * c + 128], T.PSB[:, L0:L0 + 128], float(c), -float(BIG), A.not_equal, A.mult), ["B3"], ["AM%d" % c])
-    for c in range(4):
-        V("tt", (T.QTB[:, c:512:4], T.PSB[:, L0 + 128:L0 + 256], T.AM[:, 128 * c:128 * c + 128], A.add), ["B3", "AM%d" % c], ["B3", "QTB%d" % c])
+    mms(cs, ["LTR0", "LTR1", "SELL", "PTB", "ID", "B3z"], ["B3"])
 
-    for i, k in enumerate((-1.0, -28.0, -896.0, 4096.0)):
-        V("ts", (T.HK[:, 128 * i:128 * i + 128], T.ID[:], k, None, A.mult), ["ID"], ["HK"])
-    V("memset", (T.ONE2[:], 1.0), [], ["ONE2"])
-    V("memset", (T.MK[:], 1.0), [], ["MK0"])
-    V("memset", (T.ONE32[:], 1.0), [], ["ONE32"])
-    V("memset", (T.BASE[:, 0:1], 0.0), [], ["BASE0"])
-    V("memset", (T.TB[:, 3:2048:4], 0.0), [], ["TB3"])
-    V("memset", (T.RST[:], 1.0), [], ["RST0"])
-    V("memset", (T.MK[:, 0:512:16], 0.0), ["MK0"], ["MK"])
-    V("memset", (T.RST[:, 0:64:4], 0.0), ["RST0"], ["RST"])
-    V("ts", (T.IDN[:], T.ID[:], -1.0, None, A.mult), ["ID"], ["IDN"])
-    V("ts", (T.OFF[:], T.G5[:], col(23), None, A.add), ["G5", "K23"], ["OFF"])
-    V("ts", (T.EM[:, 0:4], T.IC4[:], col(3), None, A.is_equal), ["IC4", "KF"], ["EM"])
-    for c in range(4):
-        V("ts", (T.SELY[:, c:32:4], T.GB[:, c:32:4], col(8), T.EM[:, c:c + 1], A.mult, A.mult), ["GB", "K8", "EM"], ["SELY%d" % c])
-        V("ts", (T.SELZ[:, c:32:4], T.GB[:, c:32:4], col(25), T.EM[:, c:c + 1], A.mult, A.mult), ["GB", "K25", "EM"], ["SELZ%d" % c])
-    op("g", "asel", (T.TRI[:], T.ONE1[:], [[1, 128]], A.is_ge, 0.0, -1, -1), ["ONE1"], ["TRI"])
-    op("g", "asel", (T.SEL[:], T.ONE2[:], [[-16, 8], [0, 8], [-1, 16]], A.is_equal, 0.0, 0, 1), ["ONE2"], ["SEL"])
+    V("copy", (T.CI[:], T.LR[:, 0:384].indirect(T.OFC[:, 0:8])), ["LR", "LRs", "OFC"], ["CI"])
+    S("act", (T.H[:], T.LR[:, 0:384].indirect(T.OFX[:, 0:16]), AF.Copy), ["LR", "LRs", "OFX"], ["H"], scale=(1.0 + 2.0 ** -17) / 256, bias=RND)
+    S("act", (T.LXP[:, 1:512:2], T.H[:], AF.Copy), ["H"], ["LXP1"], bias=-RND - 129.0)
+    LXK = ["LXP0", "LXP1"]
 
-    TAK, TBK = ["TA0", "TA1", "TA2", "TA3"], ["TB0", "TB1", "TB2", "TB3"]
-    op("a", "act", (T.LXP[:], T.LX[:, 0:512].indirect(T.OFX[:, 0:32]), AF.Copy), ["LX", "LXs", "OFX"], ["LXP"])
-    for i in range(1, 4):
-        V("ts", (T.TA[:, i:2048:4], T.LXP[:], B_T[i], 32.0 / 4 ** i, A.add, A.mult), ["LXP"], ["TA%d" % i])
-    op("a", "act", (T.TA[:, 0:2048:4], T.LXP[:], AF.Identity), ["LXP"], ["TA0"], scale=32.0)
-    mms([(T.PSB[:, 0:512], T.HK[:, 128 * i:128 * i + 128], T.TA[:, i:2048:4], i == 0, i == 3) for i in range(4)], TAK + ["HK"], ["B0"])
-    for i in range(3):
-        sc = 32.0 / 4 ** i
-        op("a", "act", (T.TB[:, i:2048:4], T.LXP[:], AF.Copy), ["LXP"], ["TB%d" % i], scale=sc, bias=sc * B_T[i + 1])
-    op("a", "act", (T.HNS[:], T.PSB[:, 0:512], AF.Identity), ["B0"], ["B0", "HNS"], bias=float(BIAS - 16240640))
+    def planes(e, lst):
+        for x in lst.split():
+            name, i = "T" + x[1], int(x[2])
+            k, sc = i + (x[1] == "B"), 64.0 / 4 ** i
+            args, wr = (T[name][:, 1024 * e + i:1024 * e + 1024:4], T.LXP[:, 256 * e:256 * e + 256]), ["%s%d%d" % (name, i, e)]
+            if x[0] == "v":
+                V("ts", args + (B_T[k] + 128.0, sc, A.add, A.mult), LXK, wr)
+            else:
+                S("act", args + (AF.Copy,), LXK, wr, scale=sc, bias=sc * (B_T[k] + 128.0))
 
-    V("copy", (T.CI[:], T.LC[:]), ["LC", "LCs"], ["CI"])
-    for c in range(4):
+    def cx(c):
         V("ts", (T.CX[:, 128 * c:128 * c + 128], T.CI[:], 5 * c, 31, A.arith_shift_right, A.bitwise_and), ["CI"], ["CX"])
+    cx(0)
+    cx(1)
+    V("ts", (T.HM[:], T.H[:], -RND, -256.0, A.add, A.mult), ["H"], ["HM"])
+    cx(2)
+    V("tt", (T.LXP[:, 0:512:2], T.LR[:, 0:384].indirect(T.OFX[:, 0:16]), T.HM[:], A.add), ["LR", "LRs", "OFX", "HM"], ["LXP0"])
+    cx(3)
     V("copy", (T.NS[:, 1:512], T.CX[:, 0:511]), ["CX"], ["NS"])
     V("copy", (T.N15[:], T.CX[:, 15:512:16]), ["CX"], ["N15"])
     V("memset", (T.NS[:, 0:512:16], 0.0), ["NS"], ["NS"])
     V("scan", (T.S1[:], T.MK[:], T.NS[:], 0.0, A.mult, A.add), ["MK", "NS"], ["S1"])
+    planes(0, P0)
     for j, (m, k) in enumerate(((T.ONE1[:], "ONE1"), (T.TRI[:], "TRI"))):
         o = T.PSB[:, 512 + 512 * j:544 + 512 * j]
         mms([(o, m, T.S1[:, 15:512:16], True, False), (o, m, T.N15[:], False, True)], ["S1", "N15", k], ["B%d" % (1 + j)])
     V("scan", (T.BASE[:, 1:33], T.ONE32[:], T.PSB[:, 512:544], 0.0, A.mult, A.add), ["B1", "ONE32"], ["B1", "BASE"])
     V("tt", (T.NS[:, 0:512:16], T.PSB[:, 1024:1056], T.BASE[:, 0:32], A.add), ["B2", "BASE", "BASE0"], ["B2", "NS"])
     V("scan", (T.F[:], T.MK[:], T.NS[:], 0.0, A.mult, A.add), ["MK", "NS"], ["F"])
-    V("tt", (T.NI[:], T.F[:, 0:512].indirect(T.OFF[:, 0:32]), T.HNS[:], A.add), ["F", "OFF", "HNS"], ["NI"])
+    planes(1, P1)
+    PO = lambda b, m: T.PSA[:, 512 * b + m:512 * b + 512:4]
 
-    for bk in range(4):
-        cs = []
-        for il in range(4 * bk, 4 * bk + 4):
-            o = T.PSA[:, 128 * il:128 * il + 128]
-            cs += [(o, T.TA[:, 128 * il:128 * il + 128], T.ID[:], True, False), (o, T.TB[:, 128 * il:128 * il + 128], T.IDN[:], False, True)]
-        mms(cs, TAK + TBK + ["ID", "IDN"], ["A%d" % bk])
-        op("a", "act", (T.XL[:, 512 * bk:512 * bk + 512], T.PSA[:, 512 * bk:512 * bk + 512], AF.Identity), ["A%d" % bk, "K18"],
-           ["A%d" % bk, "XL%d" % bk], bias=col(18))
-    for bk in range(2):
-        mms([(T.PSA[:, 512 * bk:512 * bk + 512], T.ID[:], T.XL[:, 512 * bk:512 * bk + 512], True, False)], ["XL%d" % bk, "ID"], ["A%d" % bk])
-    XCK = ["XC%d" % bk for bk in range(4)]
+    def letters_turned(e):
+        for b in (2 * e, 2 * e + 1):
+            cs = []
+            for m in range(4):
+                x0 = 128 * (4 * b + m)
+                cs += [(PO(b, m), T.TA[:, x0:x0 + 128], T.IDP[:], False, False), (PO(b, m), T.TB[:, x0:x0 + 128], T.IDN[:], False, False)]
+            mms(cs, ["TA%d%d" % (i, e) for i in range(4)] + ["TB%d%d" % (i, e) for i in range(3)] + ["TB3", "IDP", "IDN"], ["A%d" % b])
+
+    def xc(b):
+        cp(XCQ[b], T.XC[:, b:2048:4], T.PSA[:, 512 * b:512 * b + 512], ["A%d" % b], ["A%d" % b, "XC%d" % b])
+
     for e in range(2):
         n0, n1, m0, m1 = 256 * e, 256 * e + 256, 1024 * e, 1024 * e + 1024
-        V("ts", (T.DB[:, m0 + 3:m1:4], T.NI[:, n0:n1], 2.0 ** -15, 191.5 + 2.0 ** -16, A.mult, A.add), ["NI"], ["DB3%d" % e])
-        for i in range(3):
-            V("ts", (T.DI[:, 512 * i + n0:512 * i + n1], T.NI[:, n0:n1], 5 * i, 31, A.arith_shift_right, A.bitwise_and), ["NI"], ["DI%d%d" % (i, e)])
-        for i in range(3):
-            V("ts", (T.DB[:, m0 + i:m1:4], T.DI[:, 512 * i + n0:512 * i + n1], -15.5, None, A.add), ["DI%d%d" % (i, e)], ["DB%d%d" % (i, e)])
-        for bk in (2 * e, 2 * e + 1):
-            mms([(T.PSA[:, 128 * il:128 * il + 128], T.DB[:, 128 * il:128 * il + 128], T.ID[:], e == 1, e == 1 or il % 4 == 3) for il in range(4 * bk, 4 * bk + 4)],
-                ["DB%d%d" % (i, e) for i in (3, 0, 1, 2)] + ["ID"], ["A%d" % bk])
-            for il in range(4 * bk, 4 * bk + 4):
-                o, x = T.XC[:, il:2048:16], T.PSA[:, 128 * il:128 * il + 128]
-                if e == 1:
-                    V("tt", (o, x, T.XL[:, 128 * il:128 * il + 128], A.add), ["A%d" % bk, "XL%d" % bk], ["A%d" % bk, XCK[bk]])
-                else:
-                    op("a", "act", (o, x, AF.Copy), ["A%d" % bk], ["A%d" % bk, XCK[bk]])
-    XK = ["XE"]
+        V("copy", (T.NI[:, n0:n1], T.F[:, 0:512].indirect(T.OFF[:, 16 * e:16 * e + 16])), ["F", "OFF"], ["NI%d" % e])
+        letters_turned(e)
+        S("act", (T.DB[:, m0 + 2:m1:4], T.F[:, 0:512].indirect(T.OFF[:, 16 * e:16 * e + 16]), AF.Copy), ["F", "OFF"], ["DB2%d" % e],
+          scale=2.0 ** -12, bias=191.5 + 2.0 ** -13)
+        if e == 0:
+            planes(1, P2)
+        for i in range(2):
+            V("ts", (T.DI[:, 512 * i + n0:512 * i + n1], T.NI[:, n0:n1], 6 * i, 63, A.arith_shift_right, A.bitwise_and), ["NI%d" % e], ["DI%d%d" % (i, e)])
+        for i in range(2):
+            V("ts", (T.DB[:, m0 + i:m1:4], T.DI[:, 512 * i + n0:512 * i + n1], -64.0, None, A.add), ["DI%d%d" % (i, e)], ["DB%d%d" % (i, e)])
+        for b in (2 * e, 2 * e + 1):
+            mms([(PO(b, m), T.DB[:, 128 * (4 * b + m):128 * (4 * b + m) + 128], T.ID[:], False, m == 3) for m in range(4)],
+                ["DB%d%d" % (i, e) for i in range(3)] + ["DB3", "ID"], ["A%d" % b])
+            xc(b)
+    for c in range(4):
+        V("ts", (T.AM[:, 128 * c:128 * c + 128], T.PSB[:, L0:L0 + 128], float(c), -float(BIG), A.not_equal, A.mult), ["B3"], ["AM%d" % c])
+    for c in range(4):
+        V("tt", (T.QTB[:, c:512:4], T.PSB[:, L0 + 128:L0 + 256], T.AM[:, 128 * c:128 * c + 128], A.add), ["B3", "B3z", "AM%d" % c], ["QTB%d" % c])
+
+    XK, XCK = ["XE"], ["XC%d" % b for b in range(4)]
     for k in range(NPE, 8):
         for y in range(8):
             dma("s", T.X[16 * y:16 * y + 16, 2048 * k:2048 * k + 2048], T.XC[16 * k:16 * k + 16, :], "rep", XCK, ["XD%d%d" % (k, y)])
             XK.append("XD%d%d" % (k, y))
+    small = [
+        lambda: V("memset", (T.RST[:], 1.0), [], ["RST0"]),
+        lambda: V("ts", (T.EM[:, 0:4], T.IC4[:], col(3), col(31), A.is_equal, A.mult), ["IC4", "KF", "K31"], ["EM"]),
+        lambda: V("ts", (T.G3[:], T.G1[:], col(1), None, A.is_gt), ["G1", "KF"], ["G3"]),
+        lambda: V("memset", (T.RST[:, 0:64:4], 0.0), ["RST0"], ["RST"]),
+        lambda: V("ts", (col(30), T.EM[:, 0:1], 7712.0, None, A.mult), ["EM"], ["K30"]),
+        lambda: V("tt", (T.EV[:, 0:4], T.EM[:, 0:4], T.BASE[:, 8:33:8], A.mult), ["EM", "BASE"], ["EV"]),
+        lambda: V("tt", (T.W[:], T.G3[:], T.G2[:], A.mult), ["G3", "G2"], ["W"]),
+        lambda: V("ts", (T.CON[:], T.ONE1[:, 0:64], col(8), col(30), A.mult, A.mult), ["ONE1", "K8", "K30"], ["CON"]),
+        lambda: V("ts", (T.ST4[:], T.ST[:], 4.0, None, A.mult), ["ST"], ["ST4"]),
+        lambda: V("red", (T.EV[:, 4:5], T.EV[:, 0:4], AxisListType.X, A.add), ["EV"], ["EV4"]),
+        lambda: lin(9, 4, -63.0 / 64, 1.0),
+        lambda: lin(10, 5, -4095.0 / 4096, 1.0),
+    ] + [
+        lambda c=c: V("ts", (T.SELY[:, c:32:4], T.GB[:, c:32:4], col(8), T.EM[:, c:c + 1], A.mult, A.mult), ["GB", "K8", "EM"], ["SELY"]) for c in range(4)
+    ] + [
+        lambda: V("tt", (col(11), col(9), col(10), A.mult), ["K9", "K10"], ["K11"]),
+    ] + [
+        lambda h=h: V("tt", (T["I%d" % h][:], T.ST4[:, 16 * h:16 * h + 16], T.PT[:, 0:16], A.add), ["ST4", "PT"], ["I%d" % h]) for h in range(2)
+    ] + [
+        lambda: lin(12, 11, 0.5, -0.5),
+        lambda: V("ts", (T.SELZ[:], T.SELY[:], -1.25, None, A.mult), ["SELY"], ["SELZ"]),
+        lambda: lin(26, 5, 64.0, -64.0),
+        lambda: lin(27, 14, 64.0, -64.0),
+        lambda: V("ts", (T.EI[:, 0:1], T.EV[:, 4:5], col(11), col(12), A.mult, A.add), ["EV4", "K11", "K12"], ["EI0"]),
+        lambda: V("ts", (T.EI[:, 1:2], T.EI[:, 0:1], 6, None, A.arith_shift_right), ["EI0"], ["EI1"]),
+        lambda: V("ts", (T.EV[:, 6:7], T.EI[:, 1:2], col(26), col(27), A.mult, A.add), ["EI1", "K26", "K27"], ["EV6"]),
+        lambda: V("tt", (T.X[:, 16384:16385], T.EI[:, 0:1], T.EV[:, 6:7], A.add), ["EI0", "EV6"], ["XE"]),
+    ]
     n = 0
-    for k in range(NPE):
-        for j in range(4):
-            b = n % 4
-            mms([(T.PSB[:, 512 * b:512 * b + 512], T.SEL[:, 128 * k:128 * k + 128], T.XC[:, 512 * j:512 * j + 512], True, True)], XCK + ["SEL"], ["B%d" % b])
-            o, x = T.X[:, 2048 * k + 512 * j:2048 * k + 512 * j + 512], T.PSB[:, 512 * b:512 * b + 512]
-            if n % 2 == 0:
-                V("copy", (o, x), ["B%d" % b], ["B%d" % b, "X%d" % n])
-            else:
-                op("a", "act", (o, x, AF.Copy), ["B%d" % b], ["B%d" % b, "X%d" % n])
+    for b in range(4):
+        for k in range(NPE):
+            pb = n % 3
+            mms([(T.PSB[:, 512 * pb:512 * pb + 512], T.SEL[:, 128 * k:128 * k + 128], T.XC[:, b:2048:4], True, True)], ["XC%d" % b, "SEL"], ["B%d" % pb])
+            cp(XQ[n], T.X[:, 2048 * k + b:2048 * k + 2048:4], T.PSB[:, 512 * pb:512 * pb + 512], ["B%d" % pb], ["B%d" % pb, "X%d" % n])
             XK.append("X%d" % n)
+            if XQ[n] == "v":
+                for f in small[:5]:
+                    f()
+                del small[:5]
             n += 1
-            if n == 2:
-                V("ts", (T.G3[:], T.G1[:], col(1), None, A.is_gt), ["G1", "KF"], ["G3"])
-                V("ts", (T.ST4[:], T.ST[:], 4.0, None, A.mult), ["ST"], ["ST4"])
-                V("tt", (T.EV[:, 0:4], T.EM[:, 0:4], T.BASE[:, 8:33:8], A.mult), ["EM", "BASE"], ["EV"])
-            if n == 4:
-                V("tt", (T.WF[:], T.G3[:], T.G2[:], A.mult), ["G3", "G2"], ["WF"])
-                for h in range(2):
-                    V("tt", (T["I%d" % h][:], T.ST4[:, 16 * h:16 * h + 16], T.PT[:, 0:16], A.add), ["ST4", "PT"], ["I%d" % h])
-                V("red", (T.EV[:, 4:5], T.EV[:, 0:4], AxisListType.X, A.add), ["EV"], ["EV4"])
-            if n == 6:
-                V("ts", (T.W[:], T.WF[:], -1.0, None, A.add), ["WF"], ["W"])
-                V("ts", (T.EV[:, 5:6], T.EV[:, 4:5], float(BIAS), col(11), A.add, A.mult), ["EV4", "K11"], ["EV5"])
-            if n == 8:
-                V("ts", (T.EI[:, 0:1], T.EV[:, 5:6], col(12), None, A.add), ["EV5", "K12"], ["EI0"])
-            if n == 10:
-                V("ts", (T.EI[:, 1:2], T.EI[:, 0:1], 31, None, A.bitwise_and), ["EI0"], ["EI1"])
-            if n == 12:
-                V("ts", (T.X[:, 16384:16385], T.EI[:, 1:2], col(24), None, A.add), ["EI1", "K24"], ["XE"])
+    for f in small:
+        f()
 
     B = lambda name, n: T[("S1B" if name == "S" and n % 2 else "%s%d" % (name, n % 2))]
     key = lambda name, n: "%s:%d" % (name, n % 2)
     for h in range(2):
         last["I:%d" % h] = last["I%d" % h]
+    QK = ["QTB%d" % c for c in range(4)]
 
     def state(n):
         ps, pk = 512 * (n % 2), "A%d" % (n % 2)
         V("scan", (B("S", n)[:], T.RST[:], T.PSA[:, ps:ps + 64], 0.0, A.mult, A.max), [pk, "RST"], [pk, key("S", n)])
 
     def block(n):
-        o = B("OA", n)[:]
-        if n < 2:
-            V("ts", (o, B("I", n)[:], 1.0 / 64, -0.5 + 0.5 / 64, A.mult, A.add), [key("I", n)], [key("OA", n)])
-        else:
-            V("ts", (o, B("S", n)[:, 3:64:4], 1.0 / 64, -0.5 - 1.5 / 64, A.mult, A.add), [key("S", n)], [key("OA", n)])
-        op("a", "act", (B("Z", n)[:], T.X[:, 0:16385].indirect(B("OA", n)[:, 0:16]), AF.Copy), [key("OA", n)] + XK, [key("Z", n)])
+        ps, pk = 512 * (n % 2), "A%d" % (n % 2)
+        src, sk = (B("I", n)[:], key("I", n)) if n < 2 else (B("S", n)[:, 3:64:4], key("S", n))
+        V("ts", (B("OA", n)[:], src, 1.0 / 64, -0.5 + 0.5 / 64, A.mult, A.add), [sk], [key("OA", n)])
+        S("act", (B("Z", n)[:], T.X[:, 0:16385].indirect(B("OA", n)[:, 0:16]), AF.Copy), [key("OA", n)] + XK, [key("Z", n)])
+        S("act", (B("ZL", n)[:], B("Z", n)[:], AF.Copy), [key("Z", n)], [key("ZL", n)], scale=0.8, bias=12313.6)
+        mms([(T.PSA[:, ps:ps + 64], T.ONE1[:], T.CON[:], True, False)], ["ONE1", "CON"], [pk])
 
     def table(n):
-        t, ps, pk, Z = n // 2, 512 * (n % 2), "A%d" % (n % 2), B("Z", n)
+        t, ps, pk, Z, ZL = n // 2, 512 * (n % 2), "A%d" % (n % 2), B("Z", n), B("ZL", n)
         q0 = 64 * tau(t)
-        cs = [(T.PSA[:, ps:ps + 64], T.ID[:], T.QTB[:, q0:q0 + 64], True, False)]
+        cs = [(T.PSA[:, ps + 32 * k:ps + 32 * k + 32], ZL[:, 128 * k:128 * k + 128], T.SELZ[:], False, False) for k in range(2)]
+        cs += [(T.PSA[:, ps:ps + 64], T.ID[:], T.QTB[:, q0:q0 + 64], False, False)]
         cs += [(T.PSA[:, ps + 32 * k:ps + 32 * k + 32], Z[:, 128 * k:128 * k + 128], T.SELY[:], False, False) for k in range(2)]
-        mms(cs, [key("Z", n), "ID"] + ["QTB%d" % c for c in range(4)] + ["SELY%d" % c for c in range(4)], [pk])
-        V("ts", (B("ZL", n)[:], Z[:], RND, RND, A.add, A.subtract), [key("Z", n)], [key("ZL", n)])
+        mms(cs, [key("Z", n), key("ZL", n), "ID", "SELY", "SELZ"] + QK, [pk])
 
     def count(n):
         ps, pk, ZL, E = 512 * (n % 2), "A%d" % (n % 2), B("ZL", n), B("E", n)
-        mms([(T.PSA[:, ps + 32 * k:ps + 32 * k + 32], ZL[:, 128 * k:128 * k + 128], T.SELZ[:], False, False) for k in range(2)],
-            [key("ZL", n)] + ["SELZ%d" % c for c in range(4)], [pk])
         V("tt", (E[:], T.W[:, 0:64].indirect(B("OB", n)[:, 0:16]), ZL[:], A.is_equal), [key("OB", n), "W", key("ZL", n)], [key("E", n)])
         mms([(T.PSA[:, ps + 32 * k:ps + 32 * k + 32], E[:, 128 * k:128 * k + 128], T.GB[:], False, k == 1) for k in range(2)],
             [key("E", n), "GB"], [pk])
@@ -355,21 +415,21 @@ def rank_program(g, core, T, topo):
         if n >= 2:
             state(n)
         if 0 < n < 17:
-            table(n - 1)
+            V("copy", (B("OB", n - 1)[:], B("J", n - 1)[:]), [key("J", n - 1)], [key("OB", n - 1)])
         if n < 16:
             block(n)
-            if n >= 2:
-                V("ts", (B("I", n)[:], B("S", n)[:, 3:64:4], -2.0, None, A.add), [key("S", n)], [key("I", n)])
         else:
             h = n % 2
-            V("ts", (T.RES[:, 16 * h:16 * h + 16], B("S", n)[:, 3:64:4], 0.25, -0.5, A.mult, A.add), [key("S", n)], ["RES%d" % h])
+            V("ts", (T.RES[:, 16 * h:16 * h + 16], B("S", n)[:, 3:64:4], 0.25, None, A.mult), [key("S", n)], ["RES%d" % h])
         if 0 < n < 17:
+            table(n - 1)
             count(n - 1)
         if n < 16:
+            if n >= 2:
+                V("copy", (B("I", n)[:], B("S", n)[:, 3:64:4]), [key("S", n)], [key("I", n)])
             V("ts", (B("J", n)[:], B("I", n)[:], 63, None, A.bitwise_and), [key("I", n)], [key("J", n)])
-            V("copy", (B("OB", n)[:], B("J", n)[:]), [key("J", n)], [key("OB", n)])
     dma("s", T.RD[:], T.RES[:], "rd", ["RES0", "RES1"], ["RD"])
-    send(lambda d: T.RD[d], T.FL[rank], "arrF", "locF", ["RD"])
+    send("F", lambda d: T.RD[d], T.FL[rank], "arrF", "locF", ["RD"])
     r0, r1 = 16 * rank, 16 * rank + 16
     dma("s", T.y[r0:r1, :], T.RES[r0:r1, :], "yself", ["RES0", "RES1"], ["y0"])
     if rank > 0:

import numpy as np
from concourse.bass import DstId, RemoteDMATransfer
from concourse.mybir import AluOpType as A, AxisListType, ActivationFunctionType as AF

NPE = 4
BIG = 2097152
RND = 12582912.0
B_T = (0.0, 638.5, 2552.5, 10208.5)
P0 = "aA0 aA1 aB0 aA2 aB1 vA3 vB2"
P1 = "aA0 aA1 aB0"
P2 = "aA2 aB1 aA3 aB2"
XCQ = "aava"
XQ = "ava" + "avavavavavavavav" * 2

SCRATCH = {
    "PP": ("dram", [8, 128, 16], "int32"), "SS": ("dram", [8, 128, 4], "int32"),
    "PL": ("dram", [8, 128, 16], "int32"), "SL": ("dram", [8, 128, 4], "int32"),
    "RD": ("dram", [8, 128, 4], "float32"), "FL": ("dram", [8, 128, 4], "float32"),
    "PSA": ("psum", [128, 2048], "float32"), "PSB": ("psum", [128, 2048], "float32"),
}
for _n, _w, _d in (
        ("D32", 2048, "int32"), ("D", 2048, "bfloat16"), ("CE", 2048, "bfloat16"), ("SEND", 384, "float32"), ("LR", 384, "float32"),
        ("H", 256, "float32"), ("HM", 256, "float32"), ("LXP", 512, "bfloat16"),
        ("TA", 2048, "bfloat16"), ("TB", 2048, "bfloat16"), ("CI", 128, "int32"), ("CX", 512, "int32"), ("NS", 512, "float32"),
        ("S1", 512, "bfloat16"), ("N15", 32, "bfloat16"), ("MK", 512, "float32"), ("BASE", 40, "float32"),
        ("ONE32", 32, "float32"), ("F", 512, "float32"), ("NI", 512, "int32"), ("DI", 1024, "int32"),
        ("DB", 2048, "bfloat16"), ("XC", 2048, "bfloat16"), ("X", 16400, "bfloat16"),
        ("ONE1", 128, "bfloat16"), ("ONE2", 512, "bfloat16"), ("FOUR", 32, "bfloat16"), ("GA", 32, "bfloat16"), ("GB", 32, "bfloat16"),
        ("ID", 128, "bfloat16"), ("IDP", 128, "bfloat16"), ("IDN", 128, "bfloat16"), ("INI", 128, "bfloat16"), ("CON", 64, "bfloat16"),
        ("PK", 1024, "bfloat16"), ("TRI", 128, "bfloat16"), ("SEL", 128 * NPE, "bfloat16"),
        ("SELY", 32, "bfloat16"), ("SELZ", 32, "bfloat16"), ("SELL", 16, "bfloat16"),
        ("KI", 16, "int32"), ("KF", 48, "float32"), ("G1", 64, "float32"),
        ("G2", 64, "float32"), ("G3", 64, "float32"), ("G4", 16, "float32"), ("G5", 32, "float32"), ("G6", 8, "float32"), ("IC4", 4, "float32"),
        ("EM", 8, "float32"), ("EV", 8, "float32"), ("EI", 4, "int32"), ("W", 64, "bfloat16"), ("LW", 16, "bfloat16"),
        ("OFX", 16, "uint16"), ("OFF", 32, "uint16"), ("OFC", 8, "uint16"), ("PT", 128, "int32"), ("ST", 32, "int32"), ("ST4", 32, "int32"),
        ("OFP", 128, "uint16"), ("PTB", 128, "bfloat16"), ("LTR", 2048, "bfloat16"), ("AM", 512, "bfloat16"), ("QTB", 512, "bfloat16"),
        ("RST", 64, "float32"), ("RES", 32, "float32"),
        ("I0", 16, "int32"), ("J0", 16, "int32"), ("OA0", 16, "uint16"), ("OB0", 16, "uint16"), ("S0", 64, "float32"),
        ("Z0", 256, "bfloat16"), ("ZL0", 256, "bfloat16"), ("E0", 256, "bfloat16"),
        ("I1", 16, "int32"), ("J1", 16, "int32"), ("OA1", 16, "uint16"), ("OB1", 16, "uint16"), ("S1B", 64, "float32"),
        ("Z1", 256, "bfloat16"), ("ZL1", 256, "bfloat16"), ("E1", 256, "bfloat16")):
    SCRATCH[_n] = ("sbuf", [128, _w], _d)
SEMAPHORES = (["vq", "aq", "pq", "gq", "dp", "ds", "dsp", "dss", "lpt", "lst", "rep", "yself", "yout", "rd",
               "arrP", "arrS", "arrX", "arrF", "locP", "locS", "locX", "locF"] + ["b%d" % _i for _i in range(8)])


def plan(T, topo, rank, kind):
    core = T.cores[rank]
    off = [d for d in range(8) if d != rank and topo.chip(T.cores[d]) != topo.chip(core)]
    on = [d for d in range(8) if d != rank and topo.chip(T.cores[d]) == topo.chip(core)]
    off.sort(key=lambda d: (topo.same_plane(topo.chip(core), topo.chip(T.cores[d])), (d - rank) % 8))
    eo = topo.engines(core, T.cores[off[0]])
    en = [e for e in topo.engines(core, T.cores[on[0]]) if e not in eo]
    if kind == "X":
        c1 = [(d, eo[2 * i:2 * i + 2]) for i, d in enumerate(off[:4])]
        c2 = [(d, eo[4 * i:4 * i + 4]) for i, d in enumerate(off[4:])] + [(d, en[:2]) for d in on]
        return [c1, c2]
    sh = 2 if kind == "S" else 0
    return [[(d, [eo[i + sh]]) for i, d in enumerate(off)] + [(d, [en[sh // 2]]) for d in on]]


def rank_program(g, core, T, topo):
    rank = T.rank_of(core)
    if rank is None:
        return
    Q = {"v": g.vector, "a": g.scalar, "p": g.tensor, "g": g, "s": g.sync}
    QS = {"v": "vq", "a": "aq", "p": "pq", "g": "gq"}
    total, last, readers = {}, {}, {}
    known = {q: {} for q in Q}

    def wait(q, tok):
        sem, val, know = tok
        if val is None:
            val = total[sem]
        if known[q].get(sem, 0) >= val:
            return
        Q[q].wait_ge(T.sem[sem], int(val))
        known[q][sem] = val
        for s, v in know.items():
            if known[q].get(s, 0) < v:
                known[q][s] = v

    def deps(q, rd, wr):
        own = QS.get(q)
        for k in rd:
            if k in last:
                wait(q, last[k])
        for k in wr:
            for tok in readers.get(k, []) + ([last[k]] if k in last else []):
                if tok[0] != own:
                    wait(q, tok)

    def mark(tok, rd, wr):
        for k in rd:
            readers.setdefault(k, []).append(tok)
        for k in wr:
            last[k] = tok
            readers[k] = []

    def op(q, name, args, rd, wr, **kw):
        deps(q, rd, wr)
        o = Q[q]
        fn = {"copy": lambda: o.tensor_copy(*args), "tt": lambda: o.tensor_tensor(*args), "ts": lambda: o.tensor_scalar(*args),
              "memset": lambda: o.memset(*args), "red": lambda: o.tensor_reduce(*args), "scan": lambda: o.tensor_tensor_scan(*args),
              "act": lambda: o.activation(*args, **kw), "iota": lambda: o.iota(*args, **kw), "asel": lambda: o.affine_select(*args)}[name]
        s = QS[q]
        fn().then_inc(T.sem[s], 1)
        total[s] = total.get(s, 0) + 1
        mark((s, total[s], dict(known[q])), rd, wr)

    def mms(calls, rd, wr):
        deps("p", rd, wr)
        for i, a in enumerate(calls):
            ins = g.tensor.matmul(*a)
            if i == len(calls) - 1:
                ins.then_inc(T.sem.pq, 1)
        total["pq"] = total.get("pq", 0) + 1
        mark(("pq", total["pq"], dict(known["p"])), rd, wr)

    def dma(q, out, in_, sem, rd, wr):
        deps(q, rd, wr)
        Q[q].dma_start(out, in_).then_inc(T.sem[sem], 16)
        total[sem] = total.get(sem, 0) + 16
        mark((sem, None, dict(known[q])), rd, wr)

    def send(kind, src, dst, arr, loc, rd):
        deps("g", rd, [])
        for call in plan(T, topo, rank, kind):
            tr = []
            for d, es in call:
                rid, pid, _ = topo.addr(T.cores[d])
                tr.append(RemoteDMATransfer(dst_ids=[DstId(rid=rid, pnc=pid)], dma_engine_mask=sum(1 << e for e in es),
                                            remote_sem=T.sem[arr], srcs=[src(d)], dsts=[dst]))
                total[loc] = total.get(loc, 0) + len(es)
            g.remote_dma_fused(tr, local_sem=T.sem[loc])
        total[arr] = arrive[arr]
        mark((loc, total[loc], dict(known["g"])), rd, [])

    arrive = {}
    for kind, k, arr in (("P", "PL", "arrP"), ("S", "SL", "arrS"), ("X", "LR", "arrX"), ("F", "FL", "arrF")):
        arrive[arr] = sum(len(es) for r in range(8) if r != rank for call in plan(T, topo, r, kind) for d, es in call if d == rank)
        last[k] = (arr, arrive[arr], {})
    V = lambda name, args, rd, wr: op("v", name, args, rd, wr)
    S = lambda name, args, rd, wr, **kw: op("a", name, args, rd, wr, **kw)

    def cp(q, out, in_, rd, wr):
        if q == "v":
            V("copy", (out, in_), rd, wr)
        else:
            S("act", (out, in_, AF.Copy), rd, wr)

    dma("s", T.PP[:], T.pats[:], "dp", [], ["PP"])
    dma("s", T.SS[:], T.starts[:], "ds", [], ["SS"])
    for s in range(8):
        dma("s" if s in (3, 5, 6, 7) else "a", T.D32[:, 256 * s:256 * s + 256], T.bwt[s:s + 1, :], "b%d" % s, [], ["D32%d" % s])
    dma("s", T.PL[rank], T.pats[16 * rank:16 * rank + 16, :], "dsp", [], ["PLs"])
    dma("s", T.SL[rank], T.starts[16 * rank:16 * rank + 16, :], "dss", [], ["SLs"])

    fl = dict(allow_small_or_imprecise_dtypes=True)
    V("memset", (T.ONE1[:], 1.0), [], ["ONE1"])
    V("memset", (T.FOUR[:], 4.0), [], ["FOUR"])
    op("g", "iota", (T.KI[:, 0:1], [[0, 1]], 0, 1), [], ["KI0"])
    op("g", "asel", (T.ID[:], T.ONE1[:], [[-1, 128]], A.is_equal, 0.0, 0, 1), ["ONE1"], ["ID"])
    op("g", "iota", (T.G4[:], [[2, 4], [8, 4]], 0, 0), [], ["G4"], **fl)
    op("g", "iota", (T.G5[:], [[1, 4], [4, 4], [64, 2]], 0, 0), [], ["G5"], **fl)
    op("g", "iota", (T.G6[:], [[48, 8]], 32, 0), [], ["G6"], **fl)
    op("g", "iota", (T.IC4[:], [[1, 4]], 0, 0), [], ["IC4"], **fl)
    send("P", lambda d: T.PP[d], T.PL[rank], "arrP", "locP", ["PP"])
    send("S", lambda d: T.SS[d], T.SL[rank], "arrS", "locS", ["SS"])
    op("g", "asel", (T.GA[:], T.FOUR[:], [[-16, 8], [0, 4]], A.is_ge, 0.0, 0, 1), ["FOUR"], ["GA"])
    op("g", "asel", (T.GB[:], T.GA[:], [[16, 8], [0, 4]], A.is_ge, 0.0, 15, -1), ["GA"], ["GB"])
    op("g", "asel", (T.TRI[:], T.ONE1[:], [[1, 128]], A.is_ge, 0.0, -1, -1), ["ONE1"], ["TRI"])
    op("g", "iota", (T.G1[:], [[1, 16], [0, 4]], 0, 0), [], ["G1"], **fl)
    op("g", "iota", (T.G2[:], [[0, 16], [64, 4]], 12288, 0), [], ["G2"], **fl)

    col = lambda j: T.KF[:, j:j + 1]
    for d, n, sh in ((2, 3, 0), (1, 15, 0), (3, 3, 2), (4, 1, 0), (5, 1, 1), (6, 7, 1), (7, 1, 0)):
        V("ts", (T.KI[:, d:d + 1], T.KI[:, 0:1], sh, n, A.arith_shift_right, A.bitwise_and), ["KI0"], ["KI"])
    V("copy", (T.KF[:, 0:8], T.KI[:, 0:8]), ["KI", "KI0"], ["KF"])
    S("act", (col(8), col(2), AF.Exp), ["KF"], ["K8"], scale=float(np.log(64.0)))
    for i in range(8):
        V("ts", (T.PK[:, 128 * i:128 * i + 128], T.ID[:], float(4 ** i), None, A.mult), ["ID"], ["PK"])

    def lin(j, src, k1, k2):
        V("ts", (col(j), col(src), k1, k2, A.mult, A.add), ["KF"] if src < 8 else ["K%d" % src], ["K%d" % j])

    CH = 5.0 * float(np.log(2.0))
    for s in range(8):
        c0 = 256 * s
        V("copy", (T.D[:, c0:c0 + 256], T.D32[:, c0:c0 + 256]), ["D32%d" % s], ["D%d" % s])
        S("act", (T.CE[:, c0:c0 + 256], T.D[:, c0:c0 + 256], AF.Exp), ["D%d" % s], ["CE%d" % s], scale=CH)
    for f in range(4):
        lo, hi = 512 * f, 512 * f + 512
        mms([(T.PSA[:, lo:lo + 64], T.PK[:, 128 * i:128 * i + 128], T.D[:, lo + i:hi:8], i == 0, i == 7) for i in range(8)],
            ["D%d" % (2 * f), "D%d" % (2 * f + 1), "PK"], ["A%d" % f])
        if f % 2 == 1:
            hh = f // 2
            lo, hi, o = 1024 * hh, 1024 * hh + 1024, 512 * hh
            mms([(T.PSB[:, o:o + 64], T.ID[:], T.CE[:, lo + q:hi:16], q == 0, q == 15) for q in range(16)],
                ["CE%d" % s for s in range(4 * hh, 4 * hh + 4)] + ["ID"], ["B%d" % hh])
    sk = []
    for f in range(4):
        for s in (2 * f, 2 * f + 1):
            o = 512 * f + 32 * (s % 2)
            V("ts", (T.SEND[:, 48 * s:48 * s + 32], T.PSA[:, o:o + 32], 128.0, None, A.add), ["A%d" % f], ["SX%d" % s])
            sk.append("SX%d" % s)
    for hh in range(2):
        for s in (4 * hh, 4 * hh + 1, 4 * hh + 2, 4 * hh + 3):
            o = 512 * hh + 16 * (s % 4)
            cp("a" if hh == 0 else "v", T.SEND[:, 48 * s + 32:48 * s + 48], T.PSB[:, o:o + 16], ["B%d" % hh], ["SC%d" % s])
            sk.append("SC%d" % s)
    send("X", lambda d: T.SEND[:, 48 * d:48 * d + 48], T.LR[:, 48 * rank:48 * rank + 48], "arrX", "locX", sk)
    V("copy", (T.LR[:, 48 * rank:48 * rank + 48], T.SEND[:, 48 * rank:48 * rank + 48]), ["SX%d" % rank, "SC%d" % rank], ["LRs"])

    V("memset", (T.ONE2[:], 1.0), [], ["ONE2"])
    op("g", "asel", (T.SEL[:], T.ONE2[:, 0:128 * NPE], [[-16, NPE], [0, 8], [-1, 16]], A.is_equal, 0.0, 0, 1), ["ONE2"], ["SEL"])
    lin(28, 6, 48.0, 0.0)
    lin(21, 2, 128.0, 0.0)
    lin(22, 3, 16.0, 0.0)
    lin(13, 4, -12800.0, 51200.0)
    lin(16, 5, -13056.0, 0.0)
    V("tt", (col(14), col(4), col(5), A.mult), ["KF"], ["K14"])
    V("tt", (col(29), col(28), col(7), A.add), ["K28", "KF"], ["K29"])
    V("tt", (col(23), col(21), col(22), A.add), ["K21", "K22"], ["K23"])
    V("tt", (col(17), col(13), col(16), A.add), ["K13", "K16"], ["K17"])
    lin(15, 14, -38144.0, 0.0)
    lin(31, 14, -1.0, 1.0)
    V("ts", (T.OFX[:], T.G4[:], col(29), None, A.add), ["G4", "K29"], ["OFX"])
    V("ts", (T.OFC[:], T.G6[:], col(1), None, A.add), ["G6", "KF"], ["OFC"])
    V("ts", (T.OFF[:], T.G5[:], col(23), None, A.add), ["G5", "K23"], ["OFF"])
    V("tt", (col(18), col(17), col(15), A.add), ["K17", "K15"], ["K18"])
    V("memset", (T.MK[:], 1.0), [], ["MK0"])
    V("memset", (T.ONE32[:], 1.0), [], ["ONE32"])
    V("memset", (T.BASE[:, 0:1], 0.0), [], ["BASE0"])
    V("ts", (T.INI[:], T.ID[:], col(18), None, A.mult), ["ID", "K18"], ["INI"])
    V("memset", (T.TB[:, 3:2048:4], 0.0), [], ["TB3"])
    V("memset", (T.DB[:, 3:2048:4], 0.0), [], ["DB3"])
    V("ts", (T.IDP[:], T.ID[:], 1.25, None, A.mult), ["ID"], ["IDP"])
    V("ts", (T.IDN[:], T.ID[:], -1.25, None, A.mult), ["ID"], ["IDN"])
    V("memset", (T.MK[:, 0:512:16], 0.0), ["MK0"], ["MK"])
    V("copy", (T.LW[:, 0:4], T.IC4[:]), ["IC4"], ["LW"])
    V("ts", (T.SELL[:, 0:8], T.GB[:, 0:32:4], 1.0 / 64, None, A.mult), ["GB"], ["SELL"])
    L0 = 1536
    V("memset", (T.PSB[:, L0 + 240:L0 + 256], 0.0), [], ["B3z"])
    mms([(T.PSA[:, 512 * b:512 * b + 512], T.INI[:], T.ONE2[:, 0:512], True, False) for b in range(4)], ["INI", "ONE2"], ["A0", "A1", "A2", "A3"])

    dma("s", T.PT[:], T.PL[:], "lpt", ["PL", "PLs"], ["PT"])
    dma("s", T.ST[:], T.SL[:], "lst", ["SL", "SLs"], ["ST"])
    V("copy", (T.OFP[:], T.PT[:]), ["PT"], ["OFP"])
    V("copy", (T.PTB[:], T.PT[:]), ["PT"], ["PTB"])
    S("act", (T.LTR[:, 0:1024], T.LW[:, 0:4].indirect(T.OFP[:, 0:64]), AF.Copy), ["LW", "OFP"], ["LTR0"])
    V("copy", (T.LTR[:, 1024:2048], T.LW[:, 0:4].indirect(T.OFP[:, 64:128])), ["LW", "OFP"], ["LTR1"])
    tau = lambda t: t // 2 + (4 if t % 2 else 0)
    cs = []
    for t in range(8):
        o = L0 + 16 * (t // 2) + (128 if t % 2 else 0)
        for blk in range(2):
            cs.append((T.PSB[:, o + 8 * blk:o + 8 * blk + 8], T.LTR[:, 256 * t + 128 * blk:256 * t + 128 * blk + 128], T.SELL[:, 0:8], True, True))
    for t in range(1, 8):
        o = L0 + 64 + 16 * ((t - 1) // 2) + (0 if t % 2 else 128)
        cs.append((T.PSB[:, o:o + 16], T.ID[:], T.PTB[:, 16 * t:16 * t + 16], True, True))
    mms(cs, ["LTR0", "LTR1", "SELL", "PTB", "ID", "B3z"], ["B3"])

    V("copy", (T.CI[:], T.LR[:, 0:384].indirect(T.OFC[:, 0:8])), ["LR", "LRs", "OFC"], ["CI"])
    S("act", (T.H[:], T.LR[:, 0:384].indirect(T.OFX[:, 0:16]), AF.Copy), ["LR", "LRs", "OFX"], ["H"], scale=(1.0 + 2.0 ** -17) / 256, bias=RND)
    S("act", (T.LXP[:, 1:512:2], T.H[:], AF.Copy), ["H"], ["LXP1"], bias=-RND - 129.0)
    LXK = ["LXP0", "LXP1"]

    def planes(e, lst):
        for x in lst.split():
            name, i = "T" + x[1], int(x[2])
            k, sc = i + (x[1] == "B"), 64.0 / 4 ** i
            args, wr = (T[name][:, 1024 * e + i:1024 * e + 1024:4], T.LXP[:, 256 * e:256 * e + 256]), ["%s%d%d" % (name, i, e)]
            if x[0] == "v":
                V("ts", args + (B_T[k] + 128.0, sc, A.add, A.mult), LXK, wr)
            else:
                S("act", args + (AF.Copy,), LXK, wr, scale=sc, bias=sc * (B_T[k] + 128.0))

    def cx(c):
        V("ts", (T.CX[:, 128 * c:128 * c + 128], T.CI[:], 5 * c, 31, A.arith_shift_right, A.bitwise_and), ["CI"], ["CX"])
    cx(0)
    cx(1)
    V("ts", (T.HM[:], T.H[:], -RND, -256.0, A.add, A.mult), ["H"], ["HM"])
    cx(2)
    V("tt", (T.LXP[:, 0:512:2], T.LR[:, 0:384].indirect(T.OFX[:, 0:16]), T.HM[:], A.add), ["LR", "LRs", "OFX", "HM"], ["LXP0"])
    cx(3)
    V("copy", (T.NS[:, 1:512], T.CX[:, 0:511]), ["CX"], ["NS"])
    V("copy", (T.N15[:], T.CX[:, 15:512:16]), ["CX"], ["N15"])
    V("memset", (T.NS[:, 0:512:16], 0.0), ["NS"], ["NS"])
    V("scan", (T.S1[:], T.MK[:], T.NS[:], 0.0, A.mult, A.add), ["MK", "NS"], ["S1"])
    planes(0, P0)
    for j, (m, k) in enumerate(((T.ONE1[:], "ONE1"), (T.TRI[:], "TRI"))):
        o = T.PSB[:, 512 + 512 * j:544 + 512 * j]
        mms([(o, m, T.S1[:, 15:512:16], True, False), (o, m, T.N15[:], False, True)], ["S1", "N15", k], ["B%d" % (1 + j)])
    V("scan", (T.BASE[:, 1:33], T.ONE32[:], T.PSB[:, 512:544], 0.0, A.mult, A.add), ["B1", "ONE32"], ["B1", "BASE"])
    V("tt", (T.NS[:, 0:512:16], T.PSB[:, 1024:1056], T.BASE[:, 0:32], A.add), ["B2", "BASE", "BASE0"], ["B2", "NS"])
    V("scan", (T.F[:], T.MK[:], T.NS[:], 0.0, A.mult, A.add), ["MK", "NS"], ["F"])
    planes(1, P1)
    PO = lambda b, m: T.PSA[:, 512 * b + m:512 * b + 512:4]

    def letters_turned(e):
        for b in (2 * e, 2 * e + 1):
            cs = []
            for m in range(4):
                x0 = 128 * (4 * b + m)
                cs += [(PO(b, m), T.TA[:, x0:x0 + 128], T.IDP[:], False, False), (PO(b, m), T.TB[:, x0:x0 + 128], T.IDN[:], False, False)]
            mms(cs, ["TA%d%d" % (i, e) for i in range(4)] + ["TB%d%d" % (i, e) for i in range(3)] + ["TB3", "IDP", "IDN"], ["A%d" % b])

    def xc(b):
        cp(XCQ[b], T.XC[:, b:2048:4], T.PSA[:, 512 * b:512 * b + 512], ["A%d" % b], ["A%d" % b, "XC%d" % b])

    for e in range(2):
        n0, n1, m0, m1 = 256 * e, 256 * e + 256, 1024 * e, 1024 * e + 1024
        V("copy", (T.NI[:, n0:n1], T.F[:, 0:512].indirect(T.OFF[:, 16 * e:16 * e + 16])), ["F", "OFF"], ["NI%d" % e])
        letters_turned(e)
        S("act", (T.DB[:, m0 + 2:m1:4], T.F[:, 0:512].indirect(T.OFF[:, 16 * e:16 * e + 16]), AF.Copy), ["F", "OFF"], ["DB2%d" % e],
          scale=2.0 ** -12, bias=191.5 + 2.0 ** -13)
        if e == 0:
            planes(1, P2)
        for i in range(2):
            V("ts", (T.DI[:, 512 * i + n0:512 * i + n1], T.NI[:, n0:n1], 6 * i, 63, A.arith_shift_right, A.bitwise_and), ["NI%d" % e], ["DI%d%d" % (i, e)])
        for i in range(2):
            V("ts", (T.DB[:, m0 + i:m1:4], T.DI[:, 512 * i + n0:512 * i + n1], -64.0, None, A.add), ["DI%d%d" % (i, e)], ["DB%d%d" % (i, e)])
        for b in (2 * e, 2 * e + 1):
            mms([(PO(b, m), T.DB[:, 128 * (4 * b + m):128 * (4 * b + m) + 128], T.ID[:], False, m == 3) for m in range(4)],
                ["DB%d%d" % (i, e) for i in range(3)] + ["DB3", "ID"], ["A%d" % b])
            xc(b)
    for c in range(4):
        V("ts", (T.AM[:, 128 * c:128 * c + 128], T.PSB[:, L0:L0 + 128], float(c), -float(BIG), A.not_equal, A.mult), ["B3"], ["AM%d" % c])
    for c in range(4):
        V("tt", (T.QTB[:, c:512:4], T.PSB[:, L0 + 128:L0 + 256], T.AM[:, 128 * c:128 * c + 128], A.add), ["B3", "B3z", "AM%d" % c], ["QTB%d" % c])

    XK, XCK = ["XE"], ["XC%d" % b for b in range(4)]
    for k in range(NPE, 8):
        for y in range(8):
            dma("s", T.X[16 * y:16 * y + 16, 2048 * k:2048 * k + 2048], T.XC[16 * k:16 * k + 16, :], "rep", XCK, ["XD%d%d" % (k, y)])
            XK.append("XD%d%d" % (k, y))
    small = [
        lambda: V("memset", (T.RST[:], 1.0), [], ["RST0"]),
        lambda: V("ts", (T.EM[:, 0:4], T.IC4[:], col(3), col(31), A.is_equal, A.mult), ["IC4", "KF", "K31"], ["EM"]),
        lambda: V("ts", (T.G3[:], T.G1[:], col(1), None, A.is_gt), ["G1", "KF"], ["G3"]),
        lambda: V("memset", (T.RST[:, 0:64:4], 0.0), ["RST0"], ["RST"]),
        lambda: V("ts", (col(30), T.EM[:, 0:1], 7712.0, None, A.mult), ["EM"], ["K30"]),
        lambda: V("tt", (T.EV[:, 0:4], T.EM[:, 0:4], T.BASE[:, 8:33:8], A.mult), ["EM", "BASE"], ["EV"]),
        lambda: V("tt", (T.W[:], T.G3[:], T.G2[:], A.mult), ["G3", "G2"], ["W"]),
        lambda: V("ts", (T.CON[:], T.ONE1[:, 0:64], col(8), col(30), A.mult, A.mult), ["ONE1", "K8", "K30"], ["CON"]),
        lambda: V("ts", (T.ST4[:], T.ST[:], 4.0, None, A.mult), ["ST"], ["ST4"]),
        lambda: V("red", (T.EV[:, 4:5], T.EV[:, 0:4], AxisListType.X, A.add), ["EV"], ["EV4"]),
        lambda: lin(9, 4, -63.0 / 64, 1.0),
        lambda: lin(10, 5, -4095.0 / 4096, 1.0),
    ] + [
        lambda c=c: V("ts", (T.SELY[:, c:32:4], T.GB[:, c:32:4], col(8), T.EM[:, c:c + 1], A.mult, A.mult), ["GB", "K8", "EM"], ["SELY"]) for c in range(4)
    ] + [
        lambda: V("tt", (col(11), col(9), col(10), A.mult), ["K9", "K10"], ["K11"]),
    ] + [
        lambda h=h: V("tt", (T["I%d" % h][:], T.ST4[:, 16 * h:16 * h + 16], T.PT[:, 0:16], A.add), ["ST4", "PT"], ["I%d" % h]) for h in range(2)
    ] + [
        lambda: lin(12, 11, 0.5, -0.5),
        lambda: V("ts", (T.SELZ[:], T.SELY[:], -1.25, None, A.mult), ["SELY"], ["SELZ"]),
        lambda: lin(26, 5, 64.0, -64.0),
        lambda: lin(27, 14, 64.0, -64.0),
        lambda: V("ts", (T.EI[:, 0:1], T.EV[:, 4:5], col(11), col(12), A.mult, A.add), ["EV4", "K11", "K12"], ["EI0"]),
        lambda: V("ts", (T.EI[:, 1:2], T.EI[:, 0:1], 6, None, A.arith_shift_right), ["EI0"], ["EI1"]),
        lambda: V("ts", (T.EV[:, 6:7], T.EI[:, 1:2], col(26), col(27), A.mult, A.add), ["EI1", "K26", "K27"], ["EV6"]),
        lambda: V("tt", (T.X[:, 16384:16385], T.EI[:, 0:1], T.EV[:, 6:7], A.add), ["EI0", "EV6"], ["XE"]),
    ]
    n = 0
    for b in range(4):
        for k in range(NPE):
            pb = n % 3
            mms([(T.PSB[:, 512 * pb:512 * pb + 512], T.SEL[:, 128 * k:128 * k + 128], T.XC[:, b:2048:4], True, True)], ["XC%d" % b, "SEL"], ["B%d" % pb])
            cp(XQ[n], T.X[:, 2048 * k + b:2048 * k + 2048:4], T.PSB[:, 512 * pb:512 * pb + 512], ["B%d" % pb], ["B%d" % pb, "X%d" % n])
            XK.append("X%d" % n)
            if XQ[n] == "v":
                for f in small[:5]:
                    f()
                del small[:5]
            n += 1
    for f in small:
        f()

    B = lambda name, n: T[("S1B" if name == "S" and n % 2 else "%s%d" % (name, n % 2))]
    key = lambda name, n: "%s:%d" % (name, n % 2)
    for h in range(2):
        last["I:%d" % h] = last["I%d" % h]
    QK = ["QTB%d" % c for c in range(4)]

    def state(n):
        ps, pk = 512 * (n % 2), "A%d" % (n % 2)
        V("scan", (B("S", n)[:], T.RST[:], T.PSA[:, ps:ps + 64], 0.0, A.mult, A.max), [pk, "RST"], [pk, key("S", n)])

    def block(n):
        ps, pk = 512 * (n % 2), "A%d" % (n % 2)
        src, sk = (B("I", n)[:], key("I", n)) if n < 2 else (B("S", n)[:, 3:64:4], key("S", n))
        V("ts", (B("OA", n)[:], src, 1.0 / 64, -0.5 + 0.5 / 64, A.mult, A.add), [sk], [key("OA", n)])
        S("act", (B("Z", n)[:], T.X[:, 0:16385].indirect(B("OA", n)[:, 0:16]), AF.Copy), [key("OA", n)] + XK, [key("Z", n)])
        S("act", (B("ZL", n)[:], B("Z", n)[:], AF.Copy), [key("Z", n)], [key("ZL", n)], scale=0.8, bias=12313.6)
        mms([(T.PSA[:, ps:ps + 64], T.ONE1[:], T.CON[:], True, False)], ["ONE1", "CON"], [pk])

    def table(n):
        t, ps, pk, Z, ZL = n // 2, 512 * (n % 2), "A%d" % (n % 2), B("Z", n), B("ZL", n)
        q0 = 64 * tau(t)
        cs = [(T.PSA[:, ps + 32 * k:ps + 32 * k + 32], ZL[:, 128 * k:128 * k + 128], T.SELZ[:], False, False) for k in range(2)]
        cs += [(T.PSA[:, ps:ps + 64], T.ID[:], T.QTB[:, q0:q0 + 64], False, False)]
        cs += [(T.PSA[:, ps + 32 * k:ps + 32 * k + 32], Z[:, 128 * k:128 * k + 128], T.SELY[:], False, False) for k in range(2)]
        mms(cs, [key("Z", n), key("ZL", n), "ID", "SELY", "SELZ"] + QK, [pk])

    def count(n):
        ps, pk, ZL, E = 512 * (n % 2), "A%d" % (n % 2), B("ZL", n), B("E", n)
        V("tt", (E[:], T.W[:, 0:64].indirect(B("OB", n)[:, 0:16]), ZL[:], A.is_equal), [key("OB", n), "W", key("ZL", n)], [key("E", n)])
        mms([(T.PSA[:, ps + 32 * k:ps + 32 * k + 32], E[:, 128 * k:128 * k + 128], T.GB[:], False, k == 1) for k in range(2)],
            [key("E", n), "GB"], [pk])

    for n in range(18):
        if n >= 2:
            state(n)
        if 0 < n < 17:
            V("copy", (B("OB", n - 1)[:], B("J", n - 1)[:]), [key("J", n - 1)], [key("OB", n - 1)])
        if n < 16:
            block(n)
        else:
            h = n % 2
            V("ts", (T.RES[:, 16 * h:16 * h + 16], B("S", n)[:, 3:64:4], 0.25, None, A.mult), [key("S", n)], ["RES%d" % h])
        if 0 < n < 17:
            table(n - 1)
            count(n - 1)
        if n < 16:
            if n >= 2:
                V("copy", (B("I", n)[:], B("S", n)[:, 3:64:4]), [key("S", n)], [key("I", n)])
            V("ts", (B("J", n)[:], B("I", n)[:], 63, None, A.bitwise_and), [key("I", n)], [key("J", n)])
    dma("s", T.RD[:], T.RES[:], "rd", ["RES0", "RES1"], ["RD"])
    send("F", lambda d: T.RD[d], T.FL[rank], "arrF", "locF", ["RD"])
    r0, r1 = 16 * rank, 16 * rank + 16
    dma("s", T.y[r0:r1, :], T.RES[r0:r1, :], "yself", ["RES0", "RES1"], ["y0"])
    if rank > 0:
        dma("s", T.y[0:r0, :], T.FL[0:rank], "yout", ["FL"], ["y1"])
    if rank < 7:
        dma("s", T.y[r1:128, :], T.FL[rank + 1:8], "yout", ["FL"], ["y2"])
    for sem in sorted(total):
        wait("g", (sem, total[sem], {}))
